import numpy as np
import ml_dtypes


def mxq(x, axis, fmt="e4m3"):
    dtype, down = {"e4m3": (ml_dtypes.float8_e4m3fn, 7), "e5m2": (ml_dtypes.float8_e5m2, 14)}[fmt]
    v = np.moveaxis(np.asarray(x, np.float32).astype(ml_dtypes.bfloat16).astype(np.float64), axis, -1)
    blocks = v.reshape(v.shape[:-1] + (-1, 32))
    amax = np.abs(blocks).max(-1, keepdims=True)
    byte = np.maximum(np.where(amax > 0, np.frexp(amax)[1] - 1 + 127, 0) - down, 1)
    scale = np.exp2(byte - 127.0)
    codes = (blocks / scale).astype(np.float32).astype(dtype).astype(np.float64)
    return np.moveaxis((codes * scale).reshape(v.shape), -1, axis)


WIDE = False


def mx_kscale(k):
    if not WIDE:
        return np.ones(k)
    levels = np.array([10, -10, 5, -5, 0])
    if k % 512:
        return np.exp2(np.random.permutation(np.resize(levels, k // 32))).repeat(32)
    a = np.empty((k // 512, 16))
    for p in range(k // 512):
        a[p, :8] = np.random.permutation(np.resize(levels, 8))
        for g in range(8):
            far = levels[np.abs(levels - a[p, g]) >= 10]
            a[p, g + 8] = far[np.random.randint(len(far))]
    return np.exp2(a.ravel()).repeat(32)


def f64(x):
    return np.asarray(x).astype(np.float64)


def striped(idx):
    return np.tile(idx.reshape(-1, 16).T, (8, 1)).astype(np.uint16)


def unstriped(offs):
    return offs[:16].T.reshape(-1).astype(np.int64)


def pack_weight(w):
    k, n = w.shape
    w = f64(np.asarray(w, np.float32).astype(ml_dtypes.bfloat16)).reshape(k // 32, 32, n)
    amax = np.abs(w).max(1)
    byte = np.clip(np.where(amax > 0, np.frexp(amax)[1] - 1 + 127 - 7, 1), 1, 254)
    scaled = (w * np.exp2(127.0 - byte)[:, None, :]).reshape(k, n).astype(np.float32)
    words = np.ascontiguousarray(scaled.reshape(k // 512, 128, 4, n).transpose(0, 1, 3, 2)).astype(ml_dtypes.float8_e4m3fn).view(np.uint8)
    return words, np.ascontiguousarray(byte.astype(np.uint8).reshape(k // 512, 16, n))


def unpack_weight(words, scales):
    g, p, n, _ = words.shape
    vals = np.ascontiguousarray(words).view(ml_dtypes.float8_e4m3fn).astype(np.float64) * np.repeat(np.exp2(scales.astype(np.float64) - 127.0), 8, axis=1)[..., None]
    return vals.transpose(0, 1, 3, 2).reshape(g * 512, n)


def planes(y):
    n, m = y.shape
    v = y.astype(np.float32).astype(ml_dtypes.bfloat16).astype(np.float64).reshape(n // 32, 32, m)
    top = np.abs(v).max(1)
    byte = np.clip(np.where(top > 0, np.frexp(top)[1] - 1 + 127 - 7, 1), 1, 254)
    codes = (v * np.exp2(127.0 - byte)[:, None, :]).reshape(n, m).astype(np.float32).astype(ml_dtypes.float8_e4m3fn).view(np.uint8)
    words = codes.reshape(n // 512, 128, 4, m).transpose(0, 1, 3, 2)
    return np.ascontiguousarray(words), np.ascontiguousarray(byte.astype(np.uint8).reshape(n // 512, 16, m))


def relu2(v):
    return np.maximum(v, 0.0) ** 2


K, T, S, J = 1024, 4096, 1024, 512


def setup_inputs():
    n = np.random.standard_normal
    s = mx_kscale(K)[:, None]
    packed_xT = pack_weight(n((K, T)) * s)
    return {
        "x_words": packed_xT[0],
        "x_scales": packed_xT[1],
        "hT": (n((K, J)) / np.sqrt(K) / s).astype(np.float32),
        "offs": striped(np.random.permutation(T)[:S]),
    }


def reference(x_words, x_scales, hT, offs):
    xq = unpack_weight(x_words, x_scales)[:, unstriped(offs)]
    hTq = mxq(f64(hT), 0, "e4m3")
    out_0 = relu2(xq.T @ hTq)
    return (out_0,) + planes(out_0)

@@ -1,0 +1,155 @@
+from contextlib import ExitStack
+
+import concourse.mybir as mybir
+
+K, T, S, J = 1024, 4096, 1024, 512
+FLOPS = 2 * K * S * J
+
+F32 = mybir.dt.float32
+BF16 = mybir.dt.bfloat16
+I32 = mybir.dt.int32
+U32 = mybir.dt.uint32
+U16 = mybir.dt.uint16
+U8 = mybir.dt.uint8
+FP8X4 = mybir.dt.float8_e4m3fn_x4
+ACT = mybir.ActivationFunctionType
+ALU = mybir.AluOpType
+
+P = 128
+PACK = 4
+PASSES = 2
+GROUPS = 2
+HALVES = 2
+GROUP = 512
+HALF = J // HALVES
+QUADS = 4
+
+
+def weave_views(dst, src):
+    return (dst.rearrange("p (c i) t -> p c t i", i=4), src.rearrange("p t (c i) -> p c t i", i=4))
+
+
+def tile_picked_zdeja_relu2_po_kernel(tc, x_words, x_scales, hT, offs, out_0, out_1, out_2):
+    nc = tc.nc
+    with ExitStack() as ctx:
+        pool = ctx.enter_context(tc.tile_pool(name="keep", bufs=1))
+        psum = ctx.enter_context(tc.psum_pool(name="psum", bufs=1))
+
+        offsets = pool.tile([P, S // 16], U16, name="offsets")
+        word_win = [pool.tile([P, T], U32, name="word_win%d" % o, align_bytes=64) for o in range(PASSES)]
+        scale_win = pool.tile([P, T], U8, name="scale_win", align_bytes=64)
+        h_raw = [[pool.tile([P, PACK, HALF], F32, name="h_raw%d%d" % (c, o), align_bytes=64) for o in range(PASSES)] for c in range(HALVES)]
+
+        nc.vector.memset(scale_win[:].bitcast(I32), 0)
+        nc.sync.dma_start(offsets[:], offs)
+
+        def load_words(o):
+            nc.sync.dma_start(word_win[o][:].bitcast(I32), x_words[o].rearrange("p n t -> p (n t)").bitcast(I32))
+
+        load_words(0)
+        for q in range(QUADS):
+            nc.sync.dma_start(scale_win[32 * q : 32 * q + 8, :].bitcast(I32), x_scales[:, 4 * q : 4 * q + 4, :].bitcast(I32))
+        load_words(1)
+        h_rows = hT.rearrange("(o p t) j -> o p t j", p=P, t=PACK)
+        for c in range(HALVES):
+            for o in range(PASSES):
+                nc.sync.dma_start(h_raw[c][o][:], h_rows[o][:, :, c * HALF : (c + 1) * HALF])
+
+        x_codes = [[pool.tile([P, PACK, P], U32, name="x_codes%d%d" % (o, g), align_bytes=64) for g in range(GROUPS)] for o in range(PASSES)]
+        scale_picked = pool.tile([P, S], U8, name="scale_picked", align_bytes=64)
+        x_planes = pool.tile([P, GROUPS, PACK, P], U8, name="x_planes", align_bytes=64)
+
+        def gather_words(o):
+            for g in range(GROUPS):
+                nc.vector.tensor_copy(
+                    x_codes[o][g][:].rearrange("p t m -> p m t"),
+                    word_win[o][:].indirect(offsets[:, g * (GROUP // 16) : (g + 1) * (GROUP // 16)]),
+                )
+
+        gather_words(0)
+        nc.vector.tensor_copy(scale_picked[:], scale_win[:].indirect(offsets[:]))
+        nc.vector.tensor_copy(x_planes[:], scale_picked[:].rearrange("p (g m t) -> p g t m", g=GROUPS, t=PACK))
+        gather_words(1)
+
+        h_woven = [[pool.tile([P, HALF, PACK], BF16, name="h_woven%d%d" % (c, o), align_bytes=64) for o in range(PASSES)] for c in range(HALVES)]
+        h_codes = [[pool.tile([P, HALF], U32, name="h_codes%d%d" % (c, o), align_bytes=64) for o in range(PASSES)] for c in range(HALVES)]
+        h_planes = [[pool.tile([P, HALF], U8, name="h_planes%d%d" % (c, o), align_bytes=64) for o in range(PASSES)] for c in range(HALVES)]
+        banks = [[psum.tile([P, J], F32, name="bank%d%d" % (g, t)) for t in range(PACK)] for g in range(GROUPS)]
+        y_planes = pool.tile([P, J], U8, name="y_planes", align_bytes=64)
+        y_rows = out_0.rearrange("(g p t) j -> g p t j", p=P, t=PACK)
+
+        def weave(on_scalar, dst, src):
+            dst, src = weave_views(dst, src)
+            if on_scalar:
+                nc.scalar.activation(dst, src, ACT.Copy)
+            else:
+                nc.vector.tensor_copy(dst, src)
+
+        def weave_h(c, o, scalar_cols):
+            if scalar_cols > 0:
+                weave(True, h_woven[c][o][:, :scalar_cols, :], h_raw[c][o][:, :, :scalar_cols])
+            if scalar_cols < HALF:
+                weave(False, h_woven[c][o][:, scalar_cols:, :], h_raw[c][o][:, :, scalar_cols:])
+
+        def quantize_h(c, o):
+            nc.vector.quantize_mx(out=h_codes[c][o][:].bitcast(FP8X4), scales=h_planes[c][o][:], in_=h_woven[c][o][:].rearrange("p j t -> p (j t)"))
+
+        def multiply(c, o, g):
+            for t in range(PACK):
+                nc.tensor.matmul_mx(
+                    out=banks[g][t][:, c * HALF : (c + 1) * HALF],
+                    lhsT=x_codes[o][g][:, t, :].bitcast(FP8X4),
+                    lhsT_scale=x_planes[4 * o : P, g, t, :],
+                    rhs=h_codes[c][o][:].bitcast(FP8X4),
+                    rhs_scale=h_planes[c][o][:],
+                    start=(o == 0),
+                    stop=(o == PASSES - 1),
+                )
+
+        def activate(c, g, vector_rows):
+            cols = slice(c * HALF, (c + 1) * HALF)
+            relu = pool.tile([P, PACK, HALF], F32, name="relu%d%d" % (c, g), align_bytes=64)
+            y = pool.tile([P, PACK, HALF], F32, name="y%d%d" % (c, g), align_bytes=64)
+            scalar_rows = PACK - vector_rows
+            for t in range(scalar_rows):
+                nc.scalar.activation(relu[:, t, :], banks[g][t][:, cols], ACT.Relu)
+            for t in range(scalar_rows, PACK):
+                nc.vector.tensor_scalar(relu[:, t, :], banks[g][t][:, cols], 0.0, None, ALU.max)
+            nc.scalar.activation(y[:, :scalar_rows, :], relu[:, :scalar_rows, :], ACT.Square)
+            if vector_rows > 0:
+                nc.vector.tensor_tensor(y[:, scalar_rows:, :], relu[:, scalar_rows:, :], relu[:, scalar_rows:, :], ALU.mult)
+            nc.sync.dma_start(y_rows[g][:, :, cols], y[:])
+            return y
+
+        def hand_on(c, g, y):
+            cols = slice(c * HALF, (c + 1) * HALF)
+            woven = pool.tile([P, HALF, PACK], BF16, name="y_woven%d%d" % (c, g), align_bytes=64)
+            codes = pool.tile([P, HALF], U32, name="y_codes%d%d" % (c, g), align_bytes=64)
+            weave(False, woven[:], y[:])
+            nc.vector.quantize_mx(out=codes[:].bitcast(FP8X4), scales=y_planes[4 * g : P, cols], in_=woven[:].rearrange("p j t -> p (j t)"))
+            nc.sync.dma_start(out_1[g][:, cols, :].rearrange("p j t -> p (j t)").bitcast(I32), codes[:].bitcast(I32))
+
+        weave_h(0, 0, HALF)
+        weave_h(0, 1, 96)
+        quantize_h(0, 0)
+        quantize_h(0, 1)
+        for o in range(PASSES):
+            for g in range(GROUPS):
+                multiply(0, o, g)
+        weave_h(1, 0, 0)
+        y00 = activate(0, 0, 1)
+        quantize_h(1, 0)
+        weave_h(1, 1, 0)
+        y01 = activate(0, 1, 1)
+        quantize_h(1, 1)
+        for g in range(GROUPS):
+            for o in range(PASSES):
+                multiply(1, o, g)
+        hand_on(0, 0, y00)
+        y10 = activate(1, 0, 1)
+        hand_on(0, 1, y01)
+        y11 = activate(1, 1, 2)
+        hand_on(1, 0, y10)
+        hand_on(1, 1, y11)
+        for q in range(QUADS):
+            nc.sync.dma_start(out_2[:, 4 * q : 4 * q + 4, :].bitcast(I32), y_planes[32 * q : 32 * q + 8, :].bitcast(I32))

@@ -33,48 +33,55 @@ def tile_picked_zdeja_relu2_po_kernel(tc, x_words, x_scales, hT, offs, out_0, ou
     nc = tc.nc
     with ExitStack() as ctx:
         pool = ctx.enter_context(tc.tile_pool(name="keep", bufs=1))
+        reuse = ctx.enter_context(tc.tile_pool(name="reuse", bufs=1))
         psum = ctx.enter_context(tc.psum_pool(name="psum", bufs=1))
 
         offsets = pool.tile([P, S // 16], U16, name="offsets")
         word_win = [pool.tile([P, T], U32, name="word_win%d" % o, align_bytes=64) for o in range(PASSES)]
         scale_win = pool.tile([P, T], U8, name="scale_win", align_bytes=64)
-        h_raw = [[pool.tile([P, PACK, HALF], F32, name="h_raw%d%d" % (c, o), align_bytes=64) for o in range(PASSES)] for c in range(HALVES)]
+        h_raw = {}
 
         nc.vector.memset(scale_win[:].bitcast(I32), 0)
-        nc.sync.dma_start(offsets[:], offs)
 
-        def load_words(o):
-            nc.sync.dma_start(word_win[o][:].bitcast(I32), x_words[o].rearrange("p n t -> p (n t)").bitcast(I32))
+        def load_words(o, lo, hi):
+            nc.sync.dma_start(word_win[o][:, lo:hi].bitcast(I32), x_words[o][:, lo:hi, :].rearrange("p n t -> p (n t)").bitcast(I32))
 
-        load_words(0)
-        for q in range(QUADS):
-            nc.sync.dma_start(scale_win[32 * q : 32 * q + 8, :].bitcast(I32), x_scales[:, 4 * q : 4 * q + 4, :].bitcast(I32))
-        load_words(1)
         h_rows = hT.rearrange("(o p t) j -> o p t j", p=P, t=PACK)
-        for c in range(HALVES):
-            for o in range(PASSES):
-                nc.sync.dma_start(h_raw[c][o][:], h_rows[o][:, :, c * HALF : (c + 1) * HALF])
 
-        x_codes = [[pool.tile([P, PACK, P], U32, name="x_codes%d%d" % (o, g), align_bytes=64) for g in range(GROUPS)] for o in range(PASSES)]
-        scale_picked = pool.tile([P, S], U8, name="scale_picked", align_bytes=64)
+        def load_h(c, o):
+            h_raw[(c, o)] = reuse.tile([P, PACK, HALF], F32, name="h_raw%d%d" % (c, o), align_bytes=64, offset=(PASSES * c + o) * PACK * HALF * 4)
+            nc.sync.dma_start(h_raw[(c, o)][:], h_rows[o][:, :, c * HALF : (c + 1) * HALF])
+
+        load_words(1, 0, 1024)
+        nc.sync.dma_start(offsets[:], offs)
+        for q in range(QUADS):
+            nc.sync.dma_start(scale_win[32 * q : 32 * q + 32 : 4, :].bitcast(I32), x_scales[:, 4 * q : 4 * q + 4, :].bitcast(I32))
+        load_words(1, 1024, T)
+        load_words(0, 0, T)
+
+        x_codes = {}
+        scale_picked = reuse.tile([P, HALVES * PASSES * PACK * HALF * 4], U8, name="scale_picked", align_bytes=64, offset=0)
+        scale_dealt = pool.tile([P, GROUPS, PACK, P], U8, name="scale_dealt", align_bytes=64)
         x_planes = pool.tile([P, GROUPS, PACK, P], U8, name="x_planes", align_bytes=64)
+        nc.vector.memset(x_planes[:].rearrange("p g t m -> p (g t m)").bitcast(I32), 0)
 
-        def gather_words(o):
-            for g in range(GROUPS):
-                nc.vector.tensor_copy(
-                    x_codes[o][g][:].rearrange("p t m -> p m t"),
-                    word_win[o][:].indirect(offsets[:, g * (GROUP // 16) : (g + 1) * (GROUP // 16)]),
-                )
+        def gather_words(o, g, tag):
+            x_codes[(o, g)] = pool.tile([P, PACK, P], U32, name="x_codes%d%d" % (o, g), tag=tag, align_bytes=64)
+            nc.vector.tensor_copy(
+                x_codes[(o, g)][:].rearrange("p t m -> p m t"),
+                word_win[o][:].indirect(offsets[:, g * (GROUP // 16) : (g + 1) * (GROUP // 16)]),
+            )
 
-        gather_words(0)
-        nc.vector.tensor_copy(scale_picked[:], scale_win[:].indirect(offsets[:]))
-        nc.vector.tensor_copy(x_planes[:], scale_picked[:].rearrange("p (g m t) -> p g t m", g=GROUPS, t=PACK))
-        gather_words(1)
-
-        h_woven = [[pool.tile([P, HALF, PACK], BF16, name="h_woven%d%d" % (c, o), align_bytes=64) for o in range(PASSES)] for c in range(HALVES)]
+        h_woven = {}
         h_codes = [[pool.tile([P, HALF], U32, name="h_codes%d%d" % (c, o), align_bytes=64) for o in range(PASSES)] for c in range(HALVES)]
         h_planes = [[pool.tile([P, HALF], U8, name="h_planes%d%d" % (c, o), align_bytes=64) for o in range(PASSES)] for c in range(HALVES)]
-        banks = [[psum.tile([P, J], F32, name="bank%d%d" % (g, t)) for t in range(PACK)] for g in range(GROUPS)]
+        banks = [psum.tile([P, 2, HALF], F32, name="bank%d" % b) for b in range(8)]
+        place = {}
+        for t in range(PACK):
+            place[(0, 0, t)] = (t, 0)
+            place[(0, 1, t)] = (4 + t // 2, t % 2)
+            place[(1, 0, t)] = (6 + t // 2, t % 2)
+            place[(1, 1, t)] = (4 + t // 2, t % 2)
         y_planes = pool.tile([P, J], U8, name="y_planes", align_bytes=64)
         y_rows = out_0.rearrange("(g p t) j -> g p t j", p=P, t=PACK)
 
@@ -86,70 +93,127 @@ def tile_picked_zdeja_relu2_po_kernel(tc, x_words, x_scales, hT, offs, out_0, ou
                 nc.vector.tensor_copy(dst, src)
 
         def weave_h(c, o, scalar_cols):
+            h_woven[(c, o)] = pool.tile([P, HALF, PACK], BF16, name="h_woven%d%d" % (c, o), tag="h_woven%d" % ((c + o) % 2), align_bytes=64)
             if scalar_cols > 0:
-                weave(True, h_woven[c][o][:, :scalar_cols, :], h_raw[c][o][:, :, :scalar_cols])
+                weave(True, h_woven[(c, o)][:, :scalar_cols, :], h_raw[(c, o)][:, :, :scalar_cols])
             if scalar_cols < HALF:
-                weave(False, h_woven[c][o][:, scalar_cols:, :], h_raw[c][o][:, :, scalar_cols:])
+                weave(False, h_woven[(c, o)][:, scalar_cols:, :], h_raw[(c, o)][:, :, scalar_cols:])
 
         def quantize_h(c, o):
-            nc.vector.quantize_mx(out=h_codes[c][o][:].bitcast(FP8X4), scales=h_planes[c][o][:], in_=h_woven[c][o][:].rearrange("p j t -> p (j t)"))
+            nc.vector.quantize_mx(out=h_codes[c][o][:].bitcast(FP8X4), scales=h_planes[c][o][:], in_=h_woven[(c, o)][:].rearrange("p j t -> p (j t)"))
 
-        def multiply(c, o, g):
-            for t in range(PACK):
-                nc.tensor.matmul_mx(
-                    out=banks[g][t][:, c * HALF : (c + 1) * HALF],
-                    lhsT=x_codes[o][g][:, t, :].bitcast(FP8X4),
-                    lhsT_scale=x_planes[4 * o : P, g, t, :],
-                    rhs=h_codes[c][o][:].bitcast(FP8X4),
-                    rhs_scale=h_planes[c][o][:],
-                    start=(o == 0),
-                    stop=(o == PASSES - 1),
-                )
+        def multiply(c, g, t, o):
+            b, side = place[(c, g, t)]
+            nc.tensor.matmul_mx(
+                out=banks[b][:, side, :],
+                lhsT=x_codes[(o, g)][:, t, :].bitcast(FP8X4),
+                lhsT_scale=x_planes[4 * o : P, g, t, :],
+                rhs=h_codes[c][o][:].bitcast(FP8X4),
+                rhs_scale=h_planes[c][o][:],
+                start=(o == 0),
+                stop=(o == PASSES - 1),
+            )
 
-        def activate(c, g, vector_rows):
-            cols = slice(c * HALF, (c + 1) * HALF)
-            relu = pool.tile([P, PACK, HALF], F32, name="relu%d%d" % (c, g), align_bytes=64)
-            y = pool.tile([P, PACK, HALF], F32, name="y%d%d" % (c, g), align_bytes=64)
-            scalar_rows = PACK - vector_rows
-            for t in range(scalar_rows):
-                nc.scalar.activation(relu[:, t, :], banks[g][t][:, cols], ACT.Relu)
-            for t in range(scalar_rows, PACK):
-                nc.vector.tensor_scalar(relu[:, t, :], banks[g][t][:, cols], 0.0, None, ALU.max)
-            nc.scalar.activation(y[:, :scalar_rows, :], relu[:, :scalar_rows, :], ACT.Square)
-            if vector_rows > 0:
-                nc.vector.tensor_tensor(y[:, scalar_rows:, :], relu[:, scalar_rows:, :], relu[:, scalar_rows:, :], ALU.mult)
-            nc.sync.dma_start(y_rows[g][:, :, cols], y[:])
-            return y
+        relu = {}
+        y = {}
+        for c in range(HALVES):
+            for g in range(GROUPS):
+                relu[(c, g)] = pool.tile([P, PACK, HALF], F32, name="relu%d%d" % (c, g), align_bytes=64)
+                y[(c, g)] = pool.tile([P, PACK, HALF], F32, name="y%d%d" % (c, g), align_bytes=64)
 
-        def hand_on(c, g, y):
+        def rectify(on_scalar, c, g, t, rows):
+            b, side = place[(c, g, t)]
+            dst, src = relu[(c, g)][:, t : t + rows, :], banks[b][:, side : side + rows, :]
+            if on_scalar:
+                nc.scalar.activation(dst, src, ACT.Relu)
+            else:
+                nc.vector.tensor_scalar(dst, src, 0.0, None, ALU.max)
+
+        def square(on_scalar, c, g, t, rows):
+            dst, src = y[(c, g)][:, t : t + rows, :], relu[(c, g)][:, t : t + rows, :]
+            if on_scalar:
+                nc.scalar.activation(dst, src, ACT.Square)
+            else:
+                nc.vector.tensor_tensor(dst, src, src, ALU.mult)
+
+        def store_y(c, g, t):
+            nc.sync.dma_start(y_rows[g][:, t : t + 2, c * HALF : (c + 1) * HALF], y[(c, g)][:, t : t + 2, :])
+
+        def hand_on(c, g, scalar_cols):
             cols = slice(c * HALF, (c + 1) * HALF)
             woven = pool.tile([P, HALF, PACK], BF16, name="y_woven%d%d" % (c, g), align_bytes=64)
             codes = pool.tile([P, HALF], U32, name="y_codes%d%d" % (c, g), align_bytes=64)
-            weave(False, woven[:], y[:])
+            if scalar_cols > 0:
+                weave(True, woven[:, :scalar_cols, :], y[(c, g)][:, :, :scalar_cols])
+            weave(False, woven[:, scalar_cols:, :], y[(c, g)][:, :, scalar_cols:])
             nc.vector.quantize_mx(out=codes[:].bitcast(FP8X4), scales=y_planes[4 * g : P, cols], in_=woven[:].rearrange("p j t -> p (j t)"))
             nc.sync.dma_start(out_1[g][:, cols, :].rearrange("p j t -> p (j t)").bitcast(I32), codes[:].bitcast(I32))
 
+        nc.vector.tensor_copy(scale_picked[:, :S], scale_win[:].indirect(offsets[:]))
+        nc.vector.tensor_copy(scale_dealt[:], scale_picked[:, :S].rearrange("p (g m t) -> p g t m", g=GROUPS, t=PACK))
+        for q in (0, 2, 1, 3):
+            nc.sync.dma_start(
+                x_planes[32 * q : 32 * q + 8].rearrange("p g t m -> p (g t m)").bitcast(I32),
+                scale_dealt[32 * q : 32 * q + 32 : 4].rearrange("p g t m -> p (g t m)").bitcast(I32),
+            )
+        for c in range(HALVES):
+            for o in range(PASSES):
+                load_h(c, o)
+        gather_words(1, 0, "x_codes10")
+        gather_words(1, 1, "x_codes11")
+        gather_words(0, 0, "x_codes00")
+        gather_words(0, 1, "x_codes01")
+        for w in range(6):
+            nc.tensor.matmul_mx(
+                out=banks[6 + w % 2][:, 0, :],
+                lhsT=x_codes[(0, 0)][:, w % PACK, :].bitcast(FP8X4),
+                lhsT_scale=x_planes[:, 0, w % PACK, :],
+                rhs=x_codes[(1, 0)][:, 0:2, :].rearrange("p t m -> p (t m)").bitcast(FP8X4),
+                rhs_scale=x_planes[4:P, 0, 0:2, :].rearrange("p t m -> p (t m)"),
+                start=True,
+                stop=True,
+            )
         weave_h(0, 0, HALF)
-        weave_h(0, 1, 96)
         quantize_h(0, 0)
+        weave_h(0, 1, 96)
         quantize_h(0, 1)
         for o in range(PASSES):
-            for g in range(GROUPS):
-                multiply(0, o, g)
-        weave_h(1, 0, 0)
-        y00 = activate(0, 0, 1)
+            for t in range(PACK):
+                multiply(0, 0, t, o)
+        for t in range(PACK):
+            for o in range(PASSES):
+                multiply(0, 1, t, o)
+        weave_h(1, 0, 80)
         quantize_h(1, 0)
         weave_h(1, 1, 0)
-        y01 = activate(0, 1, 1)
         quantize_h(1, 1)
-        for g in range(GROUPS):
+        for t in (0, 2):
+            rectify(True, 0, 0, t, 1)
+            rectify(True, 0, 0, t + 1, 1)
+            square(True, 0, 0, t, 2)
+            store_y(0, 0, t)
+        for t in range(PACK):
             for o in range(PASSES):
-                multiply(1, o, g)
-        hand_on(0, 0, y00)
-        y10 = activate(1, 0, 1)
-        hand_on(0, 1, y01)
-        y11 = activate(1, 1, 2)
-        hand_on(1, 0, y10)
-        hand_on(1, 1, y11)
+                multiply(1, 0, t, o)
+        for t in (0, 2):
+            rectify(t == 0, 0, 1, t, 2)
+            square(t == 0, 0, 1, t, 2)
+            store_y(0, 1, t)
+        for t in range(PACK):
+            for o in range(PASSES):
+                multiply(1, 1, t, o)
+        hand_on(0, 0, 0)
+        for t in (0, 2):
+            rectify(True, 1, 0, t, 2)
+            square(True, 1, 0, t, 2)
+            store_y(1, 0, t)
+        hand_on(0, 1, 0)
+        for t in (2, 0):
+            rectify(t == 0, 1, 1, t, 2)
+            square(t == 0, 1, 1, t, 2)
+            store_y(1, 1, t)
+        hand_on(1, 0, 0)
+        hand_on(1, 1, 96)
         for q in range(QUADS):
-            nc.sync.dma_start(out_2[:, 4 * q : 4 * q + 4, :].bitcast(I32), y_planes[32 * q : 32 * q + 8, :].bitcast(I32))
+            queue = nc.scalar if q % 2 == 0 else nc.sync
+            queue.dma_start(out_2[:, 4 * q : 4 * q + 4, :].bitcast(I32), y_planes[32 * q : 32 * q + 8, :].bitcast(I32))

@@ -54,8 +54,10 @@ def tile_picked_zdeja_relu2_po_kernel(tc, x_words, x_scales, hT, offs, out_0, ou
 
         load_words(1, 0, 1024)
         nc.sync.dma_start(offsets[:], offs)
-        for q in range(QUADS):
-            nc.sync.dma_start(scale_win[32 * q : 32 * q + 32 : 4, :].bitcast(I32), x_scales[:, 4 * q : 4 * q + 4, :].bitcast(I32))
+        for half in range(2):
+            for o in range(PASSES):
+                first = 64 * half + 32 * o
+                nc.sync.dma_start(scale_win[first : first + 32 : 4, :].bitcast(I32), x_scales[o, 8 * half : 8 * half + 8, :].bitcast(I32))
         load_words(1, 1024, T)
         load_words(0, 0, T)
 
@@ -107,7 +109,7 @@ def tile_picked_zdeja_relu2_po_kernel(tc, x_words, x_scales, hT, offs, out_0, ou
             nc.tensor.matmul_mx(
                 out=banks[b][:, side, :],
                 lhsT=x_codes[(o, g)][:, t, :].bitcast(FP8X4),
-                lhsT_scale=x_planes[4 * o : P, g, t, :],
+                lhsT_scale=x_planes[8 * o : P, g, t, :],
                 rhs=h_codes[c][o][:].bitcast(FP8X4),
                 rhs_scale=h_planes[c][o][:],
                 start=(o == 0),
@@ -152,9 +154,11 @@ def tile_picked_zdeja_relu2_po_kernel(tc, x_words, x_scales, hT, offs, out_0, ou
         nc.vector.tensor_copy(scale_picked[:, :S], scale_win[:].indirect(offsets[:]))
         nc.vector.tensor_copy(scale_dealt[:], scale_picked[:, :S].rearrange("p (g m t) -> p g t m", g=GROUPS, t=PACK))
         for q in (0, 2, 1, 3):
-            nc.sync.dma_start(
-                x_planes[32 * q : 32 * q + 8].rearrange("p g t m -> p (g t m)").bitcast(I32),
-                scale_dealt[32 * q : 32 * q + 32 : 4].rearrange("p g t m -> p (g t m)").bitcast(I32),
+            first = 64 * (q // 2) + 16 * (q % 2)
+            queue = nc.sync if q % 2 == 0 else nc.scalar
+            queue.dma_start(
+                x_planes[32 * q : 32 * q + 12].rearrange("p g t m -> p (g t m)").bitcast(I32),
+                scale_dealt[first : first + 48 : 4].rearrange("p g t m -> p (g t m)").bitcast(I32),
             )
         for c in range(HALVES):
             for o in range(PASSES):
@@ -169,7 +173,7 @@ def tile_picked_zdeja_relu2_po_kernel(tc, x_words, x_scales, hT, offs, out_0, ou
                 lhsT=x_codes[(0, 0)][:, w % PACK, :].bitcast(FP8X4),
                 lhsT_scale=x_planes[:, 0, w % PACK, :],
                 rhs=x_codes[(1, 0)][:, 0:2, :].rearrange("p t m -> p (t m)").bitcast(FP8X4),
-                rhs_scale=x_planes[4:P, 0, 0:2, :].rearrange("p t m -> p (t m)"),
+                rhs_scale=x_planes[8:P, 0, 0:2, :].rearrange("p t m -> p (t m)"),
                 start=True,
                 stop=True,
             )

@@ -19,10 +19,12 @@ P = 128
 PACK = 4
 PASSES = 2
 GROUPS = 2
-HALVES = 2
 GROUP = 512
-HALF = J // HALVES
 QUADS = 4
+BANK = 512
+CHUNKS = {"a": (0, 128), "b": (128, 128), "c": (256, 256)}
+HALF = 256
+KIB = 1024
 
 
 def weave_views(dst, src):
@@ -39,7 +41,6 @@ def tile_picked_zdeja_relu2_po_kernel(tc, x_words, x_scales, hT, offs, out_0, ou
         offsets = pool.tile([P, S // 16], U16, name="offsets")
         word_win = [pool.tile([P, T], U32, name="word_win%d" % o, align_bytes=64) for o in range(PASSES)]
         scale_win = pool.tile([P, T], U8, name="scale_win", align_bytes=64)
-        h_raw = {}
 
         nc.vector.memset(scale_win[:].bitcast(I32), 0)
 
@@ -47,43 +48,51 @@ def tile_picked_zdeja_relu2_po_kernel(tc, x_words, x_scales, hT, offs, out_0, ou
             nc.sync.dma_start(word_win[o][:, lo:hi].bitcast(I32), x_words[o][:, lo:hi, :].rearrange("p n t -> p (n t)").bitcast(I32))
 
         h_rows = hT.rearrange("(o p t) j -> o p t j", p=P, t=PACK)
+        h_raw = {}
+
+        raw_offset = {("a", 0): 0, ("a", 1): 2 * KIB, ("b", 0): 14 * KIB, ("b", 1): 8 * KIB, ("c", 0): 16 * KIB, ("c", 1): 20 * KIB}
 
         def load_h(c, o):
-            h_raw[(c, o)] = reuse.tile([P, PACK, HALF], F32, name="h_raw%d%d" % (c, o), align_bytes=64, offset=(PASSES * c + o) * PACK * HALF * 4)
-            nc.sync.dma_start(h_raw[(c, o)][:], h_rows[o][:, :, c * HALF : (c + 1) * HALF])
+            first, n = CHUNKS[c]
+            h_raw[(c, o)] = reuse.tile([P, PACK, n], F32, name="h_raw%s%d" % (c, o), align_bytes=64, offset=raw_offset[(c, o)])
+            nc.sync.dma_start(h_raw[(c, o)][:], h_rows[o][:, :, first : first + n])
 
-        load_words(1, 0, 1024)
+        load_words(1, 0, 1792)
         nc.sync.dma_start(offsets[:], offs)
         for half in range(2):
             for o in range(PASSES):
                 first = 64 * half + 32 * o
                 nc.sync.dma_start(scale_win[first : first + 32 : 4, :].bitcast(I32), x_scales[o, 8 * half : 8 * half + 8, :].bitcast(I32))
-        load_words(1, 1024, T)
+        load_words(1, 1792, T)
+        load_h("a", 0)
+        load_h("a", 1)
         load_words(0, 0, T)
 
         x_codes = {}
-        scale_picked = reuse.tile([P, HALVES * PASSES * PACK * HALF * 4], U8, name="scale_picked", align_bytes=64, offset=0)
+        scale_picked = reuse.tile([P, 20 * KIB], U8, name="scale_picked", align_bytes=64, offset=4 * KIB)
         scale_dealt = pool.tile([P, GROUPS, PACK, P], U8, name="scale_dealt", align_bytes=64)
         x_planes = pool.tile([P, GROUPS, PACK, P], U8, name="x_planes", align_bytes=64)
         nc.vector.memset(x_planes[:].rearrange("p g t m -> p (g t m)").bitcast(I32), 0)
 
-        def gather_words(o, g, tag):
-            x_codes[(o, g)] = pool.tile([P, PACK, P], U32, name="x_codes%d%d" % (o, g), tag=tag, align_bytes=64)
+        def gather_words(o, g, offset):
+            x_codes[(o, g)] = reuse.tile([P, PACK, P], U32, name="x_codes%d%d" % (o, g), align_bytes=64, offset=offset)
             nc.vector.tensor_copy(
                 x_codes[(o, g)][:].rearrange("p t m -> p m t"),
                 word_win[o][:].indirect(offsets[:, g * (GROUP // 16) : (g + 1) * (GROUP // 16)]),
             )
 
         h_woven = {}
-        h_codes = [[pool.tile([P, HALF], U32, name="h_codes%d%d" % (c, o), align_bytes=64) for o in range(PASSES)] for c in range(HALVES)]
-        h_planes = [[pool.tile([P, HALF], U8, name="h_planes%d%d" % (c, o), align_bytes=64) for o in range(PASSES)] for c in range(HALVES)]
-        banks = [psum.tile([P, 2, HALF], F32, name="bank%d" % b) for b in range(8)]
+        h_codes = {}
+        h_planes = {}
+        banks = [psum.tile([P, BANK], F32, name="bank%d" % b) for b in range(8)]
         place = {}
         for t in range(PACK):
-            place[(0, 0, t)] = (t, 0)
-            place[(0, 1, t)] = (4 + t // 2, t % 2)
-            place[(1, 0, t)] = (6 + t // 2, t % 2)
-            place[(1, 1, t)] = (4 + t // 2, t % 2)
+            place[("a", 0, t)] = (t // 2, (t % 2) * 128)
+            place[("a", 1, t)] = (2, t * 128)
+            place[("b", 0, t)] = (3, t * 128)
+            place[("b", 1, t)] = (4, t * 128)
+            place[("c", 0, t)] = (5 + t // 2, (t % 2) * 256)
+            place[("c", 1, t)] = ((7 + t // 2) % 8, (t % 2) * 256)
         y_planes = pool.tile([P, J], U8, name="y_planes", align_bytes=64)
         y_rows = out_0.rearrange("(g p t) j -> g p t j", p=P, t=PACK)
 
@@ -95,61 +104,100 @@ def tile_picked_zdeja_relu2_po_kernel(tc, x_words, x_scales, hT, offs, out_0, ou
                 nc.vector.tensor_copy(dst, src)
 
         def weave_h(c, o, scalar_cols):
-            h_woven[(c, o)] = pool.tile([P, HALF, PACK], BF16, name="h_woven%d%d" % (c, o), tag="h_woven%d" % ((c + o) % 2), align_bytes=64)
+            n = CHUNKS[c][1]
             if scalar_cols > 0:
-                weave(True, h_woven[(c, o)][:, :scalar_cols, :], h_raw[(c, o)][:, :, :scalar_cols])
-            if scalar_cols < HALF:
-                weave(False, h_woven[(c, o)][:, scalar_cols:, :], h_raw[(c, o)][:, :, scalar_cols:])
+                weave(True, h_woven[c][:, o, :scalar_cols, :], h_raw[(c, o)][:, :, :scalar_cols])
+            if scalar_cols < n:
+                weave(False, h_woven[c][:, o, scalar_cols:, :], h_raw[(c, o)][:, :, scalar_cols:])
 
-        def quantize_h(c, o):
-            nc.vector.quantize_mx(out=h_codes[c][o][:].bitcast(FP8X4), scales=h_planes[c][o][:], in_=h_woven[(c, o)][:].rearrange("p j t -> p (j t)"))
-
-        def multiply(c, g, t, o):
-            b, side = place[(c, g, t)]
-            nc.tensor.matmul_mx(
-                out=banks[b][:, side, :],
-                lhsT=x_codes[(o, g)][:, t, :].bitcast(FP8X4),
-                lhsT_scale=x_planes[8 * o : P, g, t, :],
-                rhs=h_codes[c][o][:].bitcast(FP8X4),
-                rhs_scale=h_planes[c][o][:],
-                start=(o == 0),
-                stop=(o == PASSES - 1),
+        def quantize_both(c):
+            n = CHUNKS[c][1]
+            codes = pool.tile([P, PASSES, n], U32, name="h_codes%s" % c, align_bytes=64)
+            planes = pool.tile([P, PASSES, n], U8, name="h_planes%s" % c, align_bytes=64)
+            nc.vector.quantize_mx(
+                out=codes[:].rearrange("p o j -> p (o j)").bitcast(FP8X4),
+                scales=planes[:].rearrange("p o j -> p (o j)"),
+                in_=h_woven[c][:].rearrange("p o j t -> p (o j t)"),
             )
+            for o in range(PASSES):
+                h_codes[(c, o)] = codes[:, o, :]
+                h_planes[(c, o)] = planes[:, o, :]
+
+        def quantize_one(c, o, offset):
+            n = CHUNKS[c][1]
+            codes = reuse.tile([P, n], U32, name="h_codes%s%d" % (c, o), align_bytes=64, offset=offset)
+            planes = pool.tile([P, n], U8, name="h_planes%s%d" % (c, o), align_bytes=64)
+            nc.vector.quantize_mx(out=codes[:].bitcast(FP8X4), scales=planes[:], in_=h_woven[c][:, o].rearrange("p j t -> p (j t)"))
+            h_codes[(c, o)] = codes[:]
+            h_planes[(c, o)] = planes[:]
+
+        def multiply(c, g):
+            n = CHUNKS[c][1]
+            for t in range(PACK):
+                b, col = place[(c, g, t)]
+                for o in range(PASSES):
+                    nc.tensor.matmul_mx(
+                        out=banks[b][:, col : col + n],
+                        lhsT=x_codes[(o, g)][:, t, :].bitcast(FP8X4),
+                        lhsT_scale=x_planes[8 * o : P, g, t, :],
+                        rhs=h_codes[(c, o)].bitcast(FP8X4),
+                        rhs_scale=h_planes[(c, o)],
+                        start=(o == 0),
+                        stop=(o == PASSES - 1),
+                    )
 
         relu = {}
+        relu_offset = {("a", 0): 10 * KIB - 64, ("a", 1): 12 * KIB - 128, ("b", 0): 8 * KIB + 64, ("b", 1): 50 * KIB, ("c", 0): 52 * KIB, ("c", 1): 56 * KIB}
         y = {}
-        for c in range(HALVES):
+        for half in range(2):
             for g in range(GROUPS):
-                relu[(c, g)] = pool.tile([P, PACK, HALF], F32, name="relu%d%d" % (c, g), align_bytes=64)
-                y[(c, g)] = pool.tile([P, PACK, HALF], F32, name="y%d%d" % (c, g), align_bytes=64)
+                y[(half, g)] = pool.tile([P, PACK, HALF], F32, name="y%d%d" % (half, g), align_bytes=64)
+
+        def y_view(c, g, t, rows):
+            first, n = CHUNKS[c]
+            return y[(first // HALF, g)][:, t : t + rows, first % HALF : first % HALF + n]
 
         def rectify(on_scalar, c, g, t, rows):
-            b, side = place[(c, g, t)]
-            dst, src = relu[(c, g)][:, t : t + rows, :], banks[b][:, side : side + rows, :]
+            n = CHUNKS[c][1]
+            b, col = place[(c, g, t)]
+            if (c, g) not in relu:
+                relu[(c, g)] = reuse.tile([P, PACK, n], F32, name="relu%s%d" % (c, g), align_bytes=64, offset=relu_offset[(c, g)])
+            dst, src = relu[(c, g)][:, t : t + rows, :].rearrange("p t j -> p (t j)"), banks[b][:, col : col + rows * n]
             if on_scalar:
                 nc.scalar.activation(dst, src, ACT.Relu)
             else:
                 nc.vector.tensor_scalar(dst, src, 0.0, None, ALU.max)
 
         def square(on_scalar, c, g, t, rows):
-            dst, src = y[(c, g)][:, t : t + rows, :], relu[(c, g)][:, t : t + rows, :]
+            dst, src = y_view(c, g, t, rows), relu[(c, g)][:, t : t + rows, :]
             if on_scalar:
                 nc.scalar.activation(dst, src, ACT.Square)
             else:
                 nc.vector.tensor_tensor(dst, src, src, ALU.mult)
 
-        def store_y(c, g, t):
-            nc.sync.dma_start(y_rows[g][:, t : t + 2, c * HALF : (c + 1) * HALF], y[(c, g)][:, t : t + 2, :])
+        def store_y(c, g, t, rows):
+            first, n = CHUNKS[c]
+            nc.sync.dma_start(y_rows[g][:, t : t + rows, first : first + n], y_view(c, g, t, rows))
 
-        def hand_on(c, g, scalar_cols):
-            cols = slice(c * HALF, (c + 1) * HALF)
-            woven = pool.tile([P, HALF, PACK], BF16, name="y_woven%d%d" % (c, g), align_bytes=64)
-            codes = pool.tile([P, HALF], U32, name="y_codes%d%d" % (c, g), align_bytes=64)
+        y_woven = {}
+        y_codes = [pool.tile([P, GROUPS, HALF], U32, name="y_codes%d" % half, align_bytes=64) for half in range(2)]
+
+        def weave_y(half, g, scalar_cols):
+            y_woven[(half, g)] = pool.tile([P, HALF, PACK], BF16, name="y_woven%d%d" % (half, g), align_bytes=64)
             if scalar_cols > 0:
-                weave(True, woven[:, :scalar_cols, :], y[(c, g)][:, :, :scalar_cols])
-            weave(False, woven[:, scalar_cols:, :], y[(c, g)][:, :, scalar_cols:])
-            nc.vector.quantize_mx(out=codes[:].bitcast(FP8X4), scales=y_planes[4 * g : P, cols], in_=woven[:].rearrange("p j t -> p (j t)"))
-            nc.sync.dma_start(out_1[g][:, cols, :].rearrange("p j t -> p (j t)").bitcast(I32), codes[:].bitcast(I32))
+                weave(True, y_woven[(half, g)][:, :scalar_cols, :], y[(half, g)][:, :, :scalar_cols])
+            weave(False, y_woven[(half, g)][:, scalar_cols:, :], y[(half, g)][:, :, scalar_cols:])
+
+        def hand_on(half, g):
+            cols = slice(half * HALF, (half + 1) * HALF)
+            nc.vector.quantize_mx(out=y_codes[half][:, g, :].bitcast(FP8X4), scales=y_planes[4 * g : P, cols], in_=y_woven[(half, g)][:].rearrange("p j t -> p (j t)"))
+
+        def store_codes(half, g, groups):
+            cols = slice(half * HALF, (half + 1) * HALF)
+            nc.sync.dma_start(
+                out_1[g : g + groups, :, cols, :].rearrange("g p j t -> p g (j t)").bitcast(I32),
+                y_codes[half][:, g : g + groups, :].bitcast(I32),
+            )
 
         nc.vector.tensor_copy(scale_picked[:, :S], scale_win[:].indirect(offsets[:]))
         nc.vector.tensor_copy(scale_dealt[:], scale_picked[:, :S].rearrange("p (g m t) -> p g t m", g=GROUPS, t=PACK))
@@ -160,64 +208,80 @@ def tile_picked_zdeja_relu2_po_kernel(tc, x_words, x_scales, hT, offs, out_0, ou
                 x_planes[32 * q : 32 * q + 12].rearrange("p g t m -> p (g t m)").bitcast(I32),
                 scale_dealt[first : first + 48 : 4].rearrange("p g t m -> p (g t m)").bitcast(I32),
             )
-        for c in range(HALVES):
+        for c in CHUNKS:
             for o in range(PASSES):
-                load_h(c, o)
-        gather_words(1, 0, "x_codes10")
-        gather_words(1, 1, "x_codes11")
-        gather_words(0, 0, "x_codes00")
-        gather_words(0, 1, "x_codes01")
-        for w in range(6):
+                if (c, o) not in h_raw:
+                    load_h(c, o)
+        gather_words(1, 0, 40 * KIB)
+        gather_words(1, 1, 42 * KIB)
+        h_woven["a"] = reuse.tile([P, PASSES, 128, PACK], BF16, name="h_woven_a", align_bytes=64, offset=24 * KIB)
+        h_woven["b"] = pool.tile([P, PASSES, 128, PACK], BF16, name="h_woven_b", align_bytes=64)
+        h_woven["c"] = reuse.tile([P, PASSES, 256, PACK], BF16, name="h_woven_c", align_bytes=64, offset=4 * KIB + 64)
+        weave_h("a", 0, 0)
+        weave_h("a", 1, 0)
+        quantize_both("a")
+        for w in range(4):
             nc.tensor.matmul_mx(
-                out=banks[6 + w % 2][:, 0, :],
-                lhsT=x_codes[(0, 0)][:, w % PACK, :].bitcast(FP8X4),
-                lhsT_scale=x_planes[:, 0, w % PACK, :],
-                rhs=x_codes[(1, 0)][:, 0:2, :].rearrange("p t m -> p (t m)").bitcast(FP8X4),
-                rhs_scale=x_planes[8:P, 0, 0:2, :].rearrange("p t m -> p (t m)"),
+                out=banks[7][:],
+                lhsT=x_codes[(1, 1)][:, w, :].bitcast(FP8X4),
+                lhsT_scale=scale_dealt[:, 1, w, :],
+                rhs=x_codes[(1, 0)][:].rearrange("p t m -> p (t m)").bitcast(FP8X4),
+                rhs_scale=scale_dealt[:, 0].rearrange("p t m -> p (t m)"),
                 start=True,
                 stop=True,
             )
-        weave_h(0, 0, HALF)
-        quantize_h(0, 0)
-        weave_h(0, 1, 96)
-        quantize_h(0, 1)
-        for o in range(PASSES):
-            for t in range(PACK):
-                multiply(0, 0, t, o)
-        for t in range(PACK):
-            for o in range(PASSES):
-                multiply(0, 1, t, o)
-        weave_h(1, 0, 80)
-        quantize_h(1, 0)
-        weave_h(1, 1, 0)
-        quantize_h(1, 1)
-        for t in (0, 2):
-            rectify(True, 0, 0, t, 1)
-            rectify(True, 0, 0, t + 1, 1)
-            square(True, 0, 0, t, 2)
-            store_y(0, 0, t)
-        for t in range(PACK):
-            for o in range(PASSES):
-                multiply(1, 0, t, o)
-        for t in (0, 2):
-            rectify(t == 0, 0, 1, t, 2)
-            square(t == 0, 0, 1, t, 2)
-            store_y(0, 1, t)
-        for t in range(PACK):
-            for o in range(PASSES):
-                multiply(1, 1, t, o)
-        hand_on(0, 0, 0)
-        for t in (0, 2):
-            rectify(True, 1, 0, t, 2)
-            square(True, 1, 0, t, 2)
-            store_y(1, 0, t)
-        hand_on(0, 1, 0)
-        for t in (2, 0):
-            rectify(t == 0, 1, 1, t, 2)
-            square(t == 0, 1, 1, t, 2)
-            store_y(1, 1, t)
-        hand_on(1, 0, 0)
-        hand_on(1, 1, 96)
+        gather_words(0, 0, 44 * KIB)
+        multiply("a", 0)
+        gather_words(0, 1, 46 * KIB)
+        multiply("a", 1)
+        weave_h("b", 0, 128)
+        weave_h("b", 1, 128)
+        quantize_both("b")
+        multiply("b", 0)
+        multiply("b", 1)
+        weave_h("c", 0, 0)
+        weave_h("c", 1, 0)
+        quantize_one("c", 0, 48 * KIB)
+        quantize_one("c", 1, 49 * KIB)
+        rectify(True, "a", 0, 0, 2)
+        rectify(True, "a", 0, 2, 2)
+        square(True, "a", 0, 0, 4)
+        store_y("a", 0, 0, 4)
+        rectify(True, "a", 1, 0, 4)
+        multiply("c", 0)
+        multiply("c", 1)
+        rectify(True, "b", 0, 0, 4)
+        square(True, "a", 1, 0, 4)
+        store_y("a", 1, 0, 4)
+        rectify(False, "b", 1, 0, 4)
+        square(True, "b", 0, 0, 4)
+        store_y("b", 0, 0, 4)
+        square(True, "b", 1, 0, 4)
+        store_y("b", 1, 0, 4)
+        rectify(False, "c", 0, 0, 2)
+        rectify(True, "c", 0, 2, 2)
+        weave_y(0, 0, 0)
+        square(False, "c", 0, 0, 2)
+        store_y("c", 0, 0, 2)
+        rectify(True, "c", 1, 0, 2)
+        hand_on(0, 0)
+        store_codes(0, 0, 1)
+        square(True, "c", 0, 2, 2)
+        store_y("c", 0, 2, 2)
+        rectify(False, "c", 1, 2, 2)
+        square(True, "c", 1, 0, 2)
+        store_y("c", 1, 0, 2)
+        weave_y(0, 1, 0)
+        square(True, "c", 1, 2, 2)
+        store_y("c", 1, 2, 2)
+        weave_y(1, 0, 0)
+        hand_on(0, 1)
+        store_codes(0, 1, 1)
+        weave_y(1, 1, 208)
+        hand_on(1, 0)
+        store_codes(1, 0, 1)
+        hand_on(1, 1)
+        store_codes(1, 1, 1)
         for q in range(QUADS):
             queue = nc.scalar if q % 2 == 0 else nc.sync
             queue.dma_start(out_2[:, 4 * q : 4 * q + 4, :].bitcast(I32), y_planes[32 * q : 32 * q + 8, :].bitcast(I32))

@@ -201,12 +201,11 @@ def tile_picked_zdeja_relu2_po_kernel(tc, x_words, x_scales, hT, offs, out_0, ou
 
         nc.vector.tensor_copy(scale_picked[:, :S], scale_win[:].indirect(offsets[:]))
         nc.vector.tensor_copy(scale_dealt[:], scale_picked[:, :S].rearrange("p (g m t) -> p g t m", g=GROUPS, t=PACK))
-        for q in (0, 2, 1, 3):
-            first = 64 * (q // 2) + 16 * (q % 2)
-            queue = nc.sync if q % 2 == 0 else nc.scalar
-            queue.dma_start(
-                x_planes[32 * q : 32 * q + 12].rearrange("p g t m -> p (g t m)").bitcast(I32),
-                scale_dealt[first : first + 48 : 4].rearrange("p g t m -> p (g t m)").bitcast(I32),
+        for q in range(QUADS):
+            first = 32 * q - 4 * (q % 2)
+            nc.sync.dma_start(
+                x_planes[first : first + 16].rearrange("p g t m -> p (g t m)").bitcast(I32),
+                scale_dealt[64 * (q // 2) : 64 * (q // 2) + 64 : 4].rearrange("p g t m -> p (g t m)").bitcast(I32),
             )
         for c in CHUNKS:
             for o in range(PASSES):
@@ -217,8 +216,8 @@ def tile_picked_zdeja_relu2_po_kernel(tc, x_words, x_scales, hT, offs, out_0, ou
         h_woven["a"] = reuse.tile([P, PASSES, 128, PACK], BF16, name="h_woven_a", align_bytes=64, offset=24 * KIB)
         h_woven["b"] = pool.tile([P, PASSES, 128, PACK], BF16, name="h_woven_b", align_bytes=64)
         h_woven["c"] = reuse.tile([P, PASSES, 256, PACK], BF16, name="h_woven_c", align_bytes=64, offset=4 * KIB + 64)
-        weave_h("a", 0, 0)
-        weave_h("a", 1, 0)
+        weave_h("a", 0, 128)
+        weave_h("a", 1, 128)
         quantize_both("a")
         for w in range(4):
             nc.tensor.matmul_mx(

@@ -147,7 +147,7 @@ def tile_picked_zdeja_relu2_po_kernel(tc, x_words, x_scales, hT, offs, out_0, ou
                     )
 
         relu = {}
-        relu_offset = {("a", 0): 10 * KIB - 64, ("a", 1): 12 * KIB - 128, ("b", 0): 8 * KIB + 64, ("b", 1): 50 * KIB, ("c", 0): 52 * KIB, ("c", 1): 56 * KIB}
+        relu_offset = {("a", 0): 10 * KIB - 64, ("a", 1): 12 * KIB - 128, ("b", 0): 8 * KIB + 64, ("b", 1): 22 * KIB, ("c", 0): 52 * KIB, ("c", 1): 56 * KIB}
         y = {}
         for half in range(2):
             for g in range(GROUPS):

@@ -135,15 +135,16 @@ def tile_picked_zdeja_relu2_po_kernel(tc, x_words, x_scales, hT, offs, out_0, ou
             n = CHUNKS[c][1]
             for t in range(PACK):
                 b, col = place[(c, g, t)]
-                for o in range(PASSES):
+                order = (1, 0) if c == "a" else (0, 1)
+                for o in order:
                     nc.tensor.matmul_mx(
                         out=banks[b][:, col : col + n],
                         lhsT=x_codes[(o, g)][:, t, :].bitcast(FP8X4),
                         lhsT_scale=x_planes[8 * o : P, g, t, :],
                         rhs=h_codes[(c, o)].bitcast(FP8X4),
                         rhs_scale=h_planes[(c, o)],
-                        start=(o == 0),
-                        stop=(o == PASSES - 1),
+                        start=(o == order[0]),
+                        stop=(o == order[1]),
                     )
 
         relu = {}
@@ -222,8 +223,8 @@ def tile_picked_zdeja_relu2_po_kernel(tc, x_words, x_scales, hT, offs, out_0, ou
         for w in range(4):
             nc.tensor.matmul_mx(
                 out=banks[7][:],
-                lhsT=x_codes[(1, 1)][:, w, :].bitcast(FP8X4),
-                lhsT_scale=scale_dealt[:, 1, w, :],
+                lhsT=h_codes[("a", w % PASSES)].bitcast(FP8X4),
+                lhsT_scale=h_planes[("a", w % PASSES)],
                 rhs=x_codes[(1, 0)][:].rearrange("p t m -> p (t m)").bitcast(FP8X4),
                 rhs_scale=scale_dealt[:, 0].rearrange("p t m -> p (t m)"),
                 start=True,

@@ -59,10 +59,7 @@ def tile_picked_zdeja_relu2_po_kernel(tc, x_words, x_scales, hT, offs, out_0, ou
 
         load_words(1, 0, 1792)
         nc.sync.dma_start(offsets[:], offs)
-        for half in range(2):
-            for o in range(PASSES):
-                first = 64 * half + 32 * o
-                nc.sync.dma_start(scale_win[first : first + 32 : 4, :].bitcast(I32), x_scales[o, 8 * half : 8 * half + 8, :].bitcast(I32))
+        nc.sync.dma_start(scale_win[0:96:3, :].bitcast(I32), x_scales.rearrange("o r n -> r o n").bitcast(I32))
         load_words(1, 1792, T)
         load_h("a", 0)
         load_h("a", 1)
@@ -72,7 +69,6 @@ def tile_picked_zdeja_relu2_po_kernel(tc, x_words, x_scales, hT, offs, out_0, ou
         scale_picked = reuse.tile([P, 20 * KIB], U8, name="scale_picked", align_bytes=64, offset=4 * KIB)
         scale_dealt = pool.tile([P, GROUPS, PACK, P], U8, name="scale_dealt", align_bytes=64)
         x_planes = pool.tile([P, GROUPS, PACK, P], U8, name="x_planes", align_bytes=64)
-        nc.vector.memset(x_planes[:].rearrange("p g t m -> p (g t m)").bitcast(I32), 0)
 
         def gather_words(o, g, offset):
             x_codes[(o, g)] = reuse.tile([P, PACK, P], U32, name="x_codes%d%d" % (o, g), align_bytes=64, offset=offset)
@@ -140,7 +136,7 @@ def tile_picked_zdeja_relu2_po_kernel(tc, x_words, x_scales, hT, offs, out_0, ou
                     nc.tensor.matmul_mx(
                         out=banks[b][:, col : col + n],
                         lhsT=x_codes[(o, g)][:, t, :].bitcast(FP8X4),
-                        lhsT_scale=x_planes[8 * o : P, g, t, :],
+                        lhsT_scale=x_planes[4 * o : P, g, t, :],
                         rhs=h_codes[(c, o)].bitcast(FP8X4),
                         rhs_scale=h_planes[(c, o)],
                         start=(o == order[0]),
@@ -202,11 +198,10 @@ def tile_picked_zdeja_relu2_po_kernel(tc, x_words, x_scales, hT, offs, out_0, ou
 
         nc.vector.tensor_copy(scale_picked[:, :S], scale_win[:].indirect(offsets[:]))
         nc.vector.tensor_copy(scale_dealt[:], scale_picked[:, :S].rearrange("p (g m t) -> p g t m", g=GROUPS, t=PACK))
-        for q in range(QUADS):
-            first = 32 * q - 4 * (q % 2)
+        for r in range(4):
             nc.sync.dma_start(
-                x_planes[first : first + 16].rearrange("p g t m -> p (g t m)").bitcast(I32),
-                scale_dealt[64 * (q // 2) : 64 * (q // 2) + 64 : 4].rearrange("p g t m -> p (g t m)").bitcast(I32),
+                x_planes[r:P:4].rearrange("p g t m -> p (g t m)").bitcast(I32),
+                scale_dealt[6 * r : 6 * r + 96 : 3].rearrange("p g t m -> p (g t m)").bitcast(I32),
             )
         for c in CHUNKS:
             for o in range(PASSES):

@@ -272,7 +272,7 @@ def tile_picked_zdeja_relu2_po_kernel(tc, x_words, x_scales, hT, offs, out_0, ou
         weave_y(1, 0, 0)
         hand_on(0, 1)
         store_codes(0, 1, 1)
-        weave_y(1, 1, 208)
+        weave_y(1, 1, 160)
         hand_on(1, 0)
         store_codes(1, 0, 1)
         hand_on(1, 1)

@@ -179,6 +179,9 @@ def tile_picked_zdeja_relu2_po_kernel(tc, x_words, x_scales, hT, offs, out_0, ou
         y_woven = {}
         y_codes = [pool.tile([P, GROUPS, HALF], U32, name="y_codes%d" % half, align_bytes=64) for half in range(2)]
 
+        def weave_part(half, g, lo, hi):
+            weave(False, y_woven[(half, g)][:, lo:hi, :], y[(half, g)][:, :, lo:hi])
+
         def weave_y(half, g, scalar_cols):
             y_woven[(half, g)] = pool.tile([P, HALF, PACK], BF16, name="y_woven%d%d" % (half, g), align_bytes=64)
             if scalar_cols > 0:
@@ -207,8 +210,10 @@ def tile_picked_zdeja_relu2_po_kernel(tc, x_words, x_scales, hT, offs, out_0, ou
             for o in range(PASSES):
                 if (c, o) not in h_raw:
                     load_h(c, o)
-        gather_words(1, 0, 40 * KIB)
-        gather_words(1, 1, 42 * KIB)
+        early_codes = reuse.tile([P, GROUPS, PACK, P], U32, name="early_codes", align_bytes=64, offset=40 * KIB)
+        nc.vector.tensor_copy(early_codes[:].rearrange("p g t m -> p g m t"), word_win[1][:].indirect(offsets[:]))
+        for g in range(GROUPS):
+            x_codes[(1, g)] = early_codes[:, g]
         h_woven["a"] = reuse.tile([P, PASSES, 128, PACK], BF16, name="h_woven_a", align_bytes=64, offset=24 * KIB)
         h_woven["b"] = pool.tile([P, PASSES, 128, PACK], BF16, name="h_woven_b", align_bytes=64)
         h_woven["c"] = reuse.tile([P, PASSES, 256, PACK], BF16, name="h_woven_c", align_bytes=64, offset=4 * KIB + 64)
@@ -220,7 +225,7 @@ def tile_picked_zdeja_relu2_po_kernel(tc, x_words, x_scales, hT, offs, out_0, ou
                 out=banks[7][:],
                 lhsT=h_codes[("a", w % PASSES)].bitcast(FP8X4),
                 lhsT_scale=h_planes[("a", w % PASSES)],
-                rhs=x_codes[(1, 0)][:].rearrange("p t m -> p (t m)").bitcast(FP8X4),
+                rhs=x_codes[(1, 0)].rearrange("p t m -> p (t m)").bitcast(FP8X4),
                 rhs_scale=scale_dealt[:, 0].rearrange("p t m -> p (t m)"),
                 start=True,
                 stop=True,
@@ -240,7 +245,8 @@ def tile_picked_zdeja_relu2_po_kernel(tc, x_words, x_scales, hT, offs, out_0, ou
         quantize_one("c", 1, 49 * KIB)
         rectify(True, "a", 0, 0, 2)
         rectify(True, "a", 0, 2, 2)
-        square(True, "a", 0, 0, 4)
+        square(True, "a", 0, 0, 2)
+        square(True, "a", 0, 2, 2)
         store_y("a", 0, 0, 4)
         rectify(True, "a", 1, 0, 4)
         multiply("c", 0)
@@ -249,13 +255,15 @@ def tile_picked_zdeja_relu2_po_kernel(tc, x_words, x_scales, hT, offs, out_0, ou
         square(True, "a", 1, 0, 4)
         store_y("a", 1, 0, 4)
         rectify(False, "b", 1, 0, 4)
+        y_woven[(0, 0)] = reuse.tile([P, HALF, PACK], BF16, name="y_woven00", align_bytes=64, offset=20 * KIB)
+        weave_part(0, 0, 0, 128)
         square(True, "b", 0, 0, 4)
         store_y("b", 0, 0, 4)
         square(True, "b", 1, 0, 4)
         store_y("b", 1, 0, 4)
         rectify(False, "c", 0, 0, 2)
         rectify(True, "c", 0, 2, 2)
-        weave_y(0, 0, 0)
+        weave_part(0, 0, 128, 256)
         square(False, "c", 0, 0, 2)
         store_y("c", 0, 0, 2)
         rectify(True, "c", 1, 0, 2)
@@ -278,5 +286,5 @@ def tile_picked_zdeja_relu2_po_kernel(tc, x_words, x_scales, hT, offs, out_0, ou
         hand_on(1, 1)
         store_codes(1, 1, 1)
         for q in range(QUADS):
-            queue = nc.scalar if q % 2 == 0 else nc.sync
+            queue = nc.scalar if q == 0 else nc.sync
             queue.dma_start(out_2[:, 4 * q : 4 * q + 4, :].bitcast(I32), y_planes[32 * q : 32 * q + 8, :].bitcast(I32))

@@ -147,11 +147,15 @@ def tile_picked_zdeja_relu2_po_kernel(tc, x_words, x_scales, hT, offs, out_0, ou
         relu_offset = {("a", 0): 10 * KIB - 64, ("a", 1): 12 * KIB - 128, ("b", 0): 8 * KIB + 64, ("b", 1): 22 * KIB, ("c", 0): 52 * KIB, ("c", 1): 56 * KIB}
         y = {}
         for half in range(2):
-            for g in range(GROUPS):
+            for g in range(1 - half, GROUPS):
                 y[(half, g)] = pool.tile([P, PACK, HALF], F32, name="y%d%d" % (half, g), align_bytes=64)
+
+        y_first = {c: pool.tile([P, PACK, 128], F32, name="y_first%s" % c, align_bytes=64) for c in "ab"}
 
         def y_view(c, g, t, rows):
             first, n = CHUNKS[c]
+            if g == 0 and c in y_first:
+                return y_first[c][:, t : t + rows, :]
             return y[(first // HALF, g)][:, t : t + rows, first % HALF : first % HALF + n]
 
         def rectify(on_scalar, c, g, t, rows):
@@ -179,8 +183,9 @@ def tile_picked_zdeja_relu2_po_kernel(tc, x_words, x_scales, hT, offs, out_0, ou
         y_woven = {}
         y_codes = [pool.tile([P, GROUPS, HALF], U32, name="y_codes%d" % half, align_bytes=64) for half in range(2)]
 
-        def weave_part(half, g, lo, hi):
-            weave(False, y_woven[(half, g)][:, lo:hi, :], y[(half, g)][:, :, lo:hi])
+        def weave_part(c):
+            first, n = CHUNKS[c]
+            weave(False, y_woven[(0, 0)][:, first : first + n, :], y_first[c][:])
 
         def weave_y(half, g, scalar_cols):
             y_woven[(half, g)] = pool.tile([P, HALF, PACK], BF16, name="y_woven%d%d" % (half, g), align_bytes=64)
@@ -256,14 +261,14 @@ def tile_picked_zdeja_relu2_po_kernel(tc, x_words, x_scales, hT, offs, out_0, ou
         store_y("a", 1, 0, 4)
         rectify(False, "b", 1, 0, 4)
         y_woven[(0, 0)] = reuse.tile([P, HALF, PACK], BF16, name="y_woven00", align_bytes=64, offset=20 * KIB)
-        weave_part(0, 0, 0, 128)
+        weave_part("a")
         square(True, "b", 0, 0, 4)
         store_y("b", 0, 0, 4)
         square(True, "b", 1, 0, 4)
         store_y("b", 1, 0, 4)
         rectify(False, "c", 0, 0, 2)
         rectify(True, "c", 0, 2, 2)
-        weave_part(0, 0, 128, 256)
+        weave_part("b")
         square(False, "c", 0, 0, 2)
         store_y("c", 0, 0, 2)
         rectify(True, "c", 1, 0, 2)

@@ -25,6 +25,8 @@ BANK = 512
 CHUNKS = {"a": (0, 128), "b": (128, 128), "c": (256, 256)}
 HALF = 256
 KIB = 1024
+EARLY_SPLIT = 1280
+LATE_SPLIT = 2560
 
 
 def weave_views(dst, src):
@@ -57,13 +59,14 @@ def tile_picked_zdeja_relu2_po_kernel(tc, x_words, x_scales, hT, offs, out_0, ou
             h_raw[(c, o)] = reuse.tile([P, PACK, n], F32, name="h_raw%s%d" % (c, o), align_bytes=64, offset=raw_offset[(c, o)])
             nc.sync.dma_start(h_raw[(c, o)][:], h_rows[o][:, :, first : first + n])
 
-        load_words(1, 0, 1792)
-        nc.sync.dma_start(offsets[:], offs)
-        nc.sync.dma_start(scale_win[0:96:3, :].bitcast(I32), x_scales.rearrange("o r n -> r o n").bitcast(I32))
-        load_words(1, 1792, T)
         load_h("a", 0)
+        load_words(1, 0, EARLY_SPLIT)
+        nc.sync.dma_start(offsets[:], offs)
+        nc.sync.dma_start(scale_win[32:96:2, :].bitcast(I32), x_scales.rearrange("o r n -> r o n").bitcast(I32))
+        load_words(1, EARLY_SPLIT, T)
+        load_words(0, 0, LATE_SPLIT)
         load_h("a", 1)
-        load_words(0, 0, T)
+        load_words(0, LATE_SPLIT, T)
 
         x_codes = {}
         scale_picked = reuse.tile([P, 20 * KIB], U8, name="scale_picked", align_bytes=64, offset=4 * KIB)
@@ -131,7 +134,7 @@ def tile_picked_zdeja_relu2_po_kernel(tc, x_words, x_scales, hT, offs, out_0, ou
             n = CHUNKS[c][1]
             for t in range(PACK):
                 b, col = place[(c, g, t)]
-                order = (1, 0) if c == "a" else (0, 1)
+                order = (0, 1)
                 for o in order:
                     nc.tensor.matmul_mx(
                         out=banks[b][:, col : col + n],
@@ -142,6 +145,20 @@ def tile_picked_zdeja_relu2_po_kernel(tc, x_words, x_scales, hT, offs, out_0, ou
                         start=(o == order[0]),
                         stop=(o == order[1]),
                     )
+
+        def multiply_first(g, o):
+            for t in range(PACK):
+                b, col = place[("a", g, t)]
+                last = col + 128 == (256 if g == 0 else 512)
+                nc.tensor.matmul_mx(
+                    out=banks[b][:, col : col + 128],
+                    lhsT=x_codes[(o, g)][:, t, :].bitcast(FP8X4),
+                    lhsT_scale=x_planes[4 * o : P, g, t, :],
+                    rhs=h_codes[("a", o)].bitcast(FP8X4),
+                    rhs_scale=h_planes[("a", o)],
+                    start=(o == 1 and col == 0),
+                    stop=(o == 0 and last),
+                )
 
         relu = {}
         relu_offset = {("a", 0): 10 * KIB - 64, ("a", 1): 12 * KIB - 128, ("b", 0): 8 * KIB + 64, ("b", 1): 22 * KIB, ("c", 0): 52 * KIB, ("c", 1): 56 * KIB}
@@ -209,7 +226,7 @@ def tile_picked_zdeja_relu2_po_kernel(tc, x_words, x_scales, hT, offs, out_0, ou
         for r in range(4):
             nc.sync.dma_start(
                 x_planes[r:P:4].rearrange("p g t m -> p (g t m)").bitcast(I32),
-                scale_dealt[6 * r : 6 * r + 96 : 3].rearrange("p g t m -> p (g t m)").bitcast(I32),
+                scale_dealt[32 + 4 * r : 96 + 4 * r : 2].rearrange("p g t m -> p (g t m)").bitcast(I32),
             )
         for c in CHUNKS:
             for o in range(PASSES):
@@ -222,23 +239,25 @@ def tile_picked_zdeja_relu2_po_kernel(tc, x_words, x_scales, hT, offs, out_0, ou
         h_woven["a"] = reuse.tile([P, PASSES, 128, PACK], BF16, name="h_woven_a", align_bytes=64, offset=24 * KIB)
         h_woven["b"] = pool.tile([P, PASSES, 128, PACK], BF16, name="h_woven_b", align_bytes=64)
         h_woven["c"] = reuse.tile([P, PASSES, 256, PACK], BF16, name="h_woven_c", align_bytes=64, offset=4 * KIB + 64)
-        weave_h("a", 0, 128)
-        weave_h("a", 1, 128)
-        quantize_both("a")
-        for w in range(4):
+        for o in range(PASSES):
+            weave_h("a", o, 128)
+            quantize_one("a", o, (50 + o) * KIB)
+        for n in (512, 256):
             nc.tensor.matmul_mx(
-                out=banks[7][:],
-                lhsT=h_codes[("a", w % PASSES)].bitcast(FP8X4),
-                lhsT_scale=h_planes[("a", w % PASSES)],
-                rhs=x_codes[(1, 0)].rearrange("p t m -> p (t m)").bitcast(FP8X4),
-                rhs_scale=scale_dealt[:, 0].rearrange("p t m -> p (t m)"),
+                out=banks[7][:, :n],
+                lhsT=h_codes[("a", 1)].bitcast(FP8X4),
+                lhsT_scale=h_planes[("a", 1)],
+                rhs=x_codes[(1, 0)].rearrange("p t m -> p (t m)")[:, :n].bitcast(FP8X4),
+                rhs_scale=scale_dealt[:, 0].rearrange("p t m -> p (t m)")[:, :n],
                 start=True,
                 stop=True,
             )
+        multiply_first(0, 1)
         gather_words(0, 0, 44 * KIB)
-        multiply("a", 0)
+        multiply_first(0, 0)
+        multiply_first(1, 1)
         gather_words(0, 1, 46 * KIB)
-        multiply("a", 1)
+        multiply_first(1, 0)
         weave_h("b", 0, 128)
         weave_h("b", 1, 128)
         quantize_both("b")

@@ -25,8 +25,7 @@ BANK = 512
 CHUNKS = {"a": (0, 128), "b": (128, 128), "c": (256, 256)}
 HALF = 256
 KIB = 1024
-EARLY_SPLIT = 1280
-LATE_SPLIT = 2560
+LATE_SPLIT = 1792
 
 
 def weave_views(dst, src):
@@ -41,8 +40,8 @@ def tile_picked_zdeja_relu2_po_kernel(tc, x_words, x_scales, hT, offs, out_0, ou
         psum = ctx.enter_context(tc.psum_pool(name="psum", bufs=1))
 
         offsets = pool.tile([P, S // 16], U16, name="offsets")
-        word_win = [pool.tile([P, T], U32, name="word_win%d" % o, align_bytes=64) for o in range(PASSES)]
-        scale_win = pool.tile([P, T], U8, name="scale_win", align_bytes=64)
+        word_win = [pool.tile([P, T], U32, name="word_win%d" % o, align_bytes=256) for o in range(PASSES)]
+        scale_win = pool.tile([P, T], U8, name="scale_win", align_bytes=256)
 
         nc.vector.memset(scale_win[:].bitcast(I32), 0)
 
@@ -56,22 +55,21 @@ def tile_picked_zdeja_relu2_po_kernel(tc, x_words, x_scales, hT, offs, out_0, ou
 
         def load_h(c, o):
             first, n = CHUNKS[c]
-            h_raw[(c, o)] = reuse.tile([P, PACK, n], F32, name="h_raw%s%d" % (c, o), align_bytes=64, offset=raw_offset[(c, o)])
+            h_raw[(c, o)] = reuse.tile([P, PACK, n], F32, name="h_raw%s%d" % (c, o), align_bytes=256, offset=raw_offset[(c, o)])
             nc.sync.dma_start(h_raw[(c, o)][:], h_rows[o][:, :, first : first + n])
 
         load_h("a", 0)
-        load_words(1, 0, EARLY_SPLIT)
+        load_words(0, 0, LATE_SPLIT)
         nc.sync.dma_start(offsets[:], offs)
         nc.sync.dma_start(scale_win[32:96:2, :].bitcast(I32), x_scales.rearrange("o r n -> r o n").bitcast(I32))
-        load_words(1, EARLY_SPLIT, T)
-        load_words(0, 0, LATE_SPLIT)
+        load_words(1, 0, T)
         load_h("a", 1)
         load_words(0, LATE_SPLIT, T)
 
         x_codes = {}
         scale_picked = reuse.tile([P, 20 * KIB], U8, name="scale_picked", align_bytes=64, offset=4 * KIB)
-        scale_dealt = pool.tile([P, GROUPS, PACK, P], U8, name="scale_dealt", align_bytes=64)
-        x_planes = pool.tile([P, GROUPS, PACK, P], U8, name="x_planes", align_bytes=64)
+        scale_dealt = pool.tile([P, GROUPS, PACK, P], U8, name="scale_dealt", align_bytes=256)
+        x_planes = pool.tile([P, GROUPS, PACK, P], U8, name="x_planes", align_bytes=256)
 
         def gather_words(o, g, offset):
             x_codes[(o, g)] = reuse.tile([P, PACK, P], U32, name="x_codes%d%d" % (o, g), align_bytes=64, offset=offset)
@@ -92,7 +90,7 @@ def tile_picked_zdeja_relu2_po_kernel(tc, x_words, x_scales, hT, offs, out_0, ou
             place[("b", 1, t)] = (4, t * 128)
             place[("c", 0, t)] = (5 + t // 2, (t % 2) * 256)
             place[("c", 1, t)] = ((7 + t // 2) % 8, (t % 2) * 256)
-        y_planes = pool.tile([P, J], U8, name="y_planes", align_bytes=64)
+        y_planes = pool.tile([P, J], U8, name="y_planes", align_bytes=256)
         y_rows = out_0.rearrange("(g p t) j -> g p t j", p=P, t=PACK)
 
         def weave(on_scalar, dst, src):
@@ -165,9 +163,9 @@ def tile_picked_zdeja_relu2_po_kernel(tc, x_words, x_scales, hT, offs, out_0, ou
         y = {}
         for half in range(2):
             for g in range(1 - half, GROUPS):
-                y[(half, g)] = pool.tile([P, PACK, HALF], F32, name="y%d%d" % (half, g), align_bytes=64)
+                y[(half, g)] = pool.tile([P, PACK, HALF], F32, name="y%d%d" % (half, g), align_bytes=256)
 
-        y_first = {c: pool.tile([P, PACK, 128], F32, name="y_first%s" % c, align_bytes=64) for c in "ab"}
+        y_first = {c: pool.tile([P, PACK, 128], F32, name="y_first%s" % c, align_bytes=256) for c in "ab"}
 
         def y_view(c, g, t, rows):
             first, n = CHUNKS[c]
@@ -198,7 +196,7 @@ def tile_picked_zdeja_relu2_po_kernel(tc, x_words, x_scales, hT, offs, out_0, ou
             nc.sync.dma_start(y_rows[g][:, t : t + rows, first : first + n], y_view(c, g, t, rows))
 
         y_woven = {}
-        y_codes = [pool.tile([P, GROUPS, HALF], U32, name="y_codes%d" % half, align_bytes=64) for half in range(2)]
+        y_codes = [pool.tile([P, GROUPS, HALF], U32, name="y_codes%d" % half, align_bytes=256) for half in range(2)]
 
         def weave_part(c):
             first, n = CHUNKS[c]

@@ -67,12 +67,12 @@ def tile_picked_zdeja_relu2_po_kernel(tc, x_words, x_scales, hT, offs, out_0, ou
         load_words(0, LATE_SPLIT, T)
 
         x_codes = {}
-        scale_picked = reuse.tile([P, 20 * KIB], U8, name="scale_picked", align_bytes=64, offset=4 * KIB)
+        scale_picked = reuse.tile([P, 20 * KIB], U8, name="scale_picked", align_bytes=256, offset=4 * KIB)
         scale_dealt = pool.tile([P, GROUPS, PACK, P], U8, name="scale_dealt", align_bytes=256)
         x_planes = pool.tile([P, GROUPS, PACK, P], U8, name="x_planes", align_bytes=256)
 
         def gather_words(o, g, offset):
-            x_codes[(o, g)] = reuse.tile([P, PACK, P], U32, name="x_codes%d%d" % (o, g), align_bytes=64, offset=offset)
+            x_codes[(o, g)] = reuse.tile([P, PACK, P], U32, name="x_codes%d%d" % (o, g), align_bytes=256, offset=offset)
             nc.vector.tensor_copy(
                 x_codes[(o, g)][:].rearrange("p t m -> p m t"),
                 word_win[o][:].indirect(offsets[:, g * (GROUP // 16) : (g + 1) * (GROUP // 16)]),
@@ -88,9 +88,9 @@ def tile_picked_zdeja_relu2_po_kernel(tc, x_words, x_scales, hT, offs, out_0, ou
             place[("a", 1, t)] = (2, t * 128)
             place[("b", 0, t)] = (3, t * 128)
             place[("b", 1, t)] = (4, t * 128)
-            place[("c", 0, t)] = (5 + t // 2, (t % 2) * 256)
-            place[("c", 1, t)] = ((7 + t // 2) % 8, (t % 2) * 256)
-        y_planes = pool.tile([P, J], U8, name="y_planes", align_bytes=256)
+            place[("c", 1, t)] = (5 + t // 2, (t % 2) * 256)
+            place[("c", 0, t)] = ((7 + t // 2) % 8, (t % 2) * 256)
+        y_planes = pool.tile([P, GROUPS, J], U8, name="y_planes", align_bytes=256)
         y_rows = out_0.rearrange("(g p t) j -> g p t j", p=P, t=PACK)
 
         def weave(on_scalar, dst, src):
@@ -109,8 +109,8 @@ def tile_picked_zdeja_relu2_po_kernel(tc, x_words, x_scales, hT, offs, out_0, ou
 
         def quantize_both(c):
             n = CHUNKS[c][1]
-            codes = pool.tile([P, PASSES, n], U32, name="h_codes%s" % c, align_bytes=64)
-            planes = pool.tile([P, PASSES, n], U8, name="h_planes%s" % c, align_bytes=64)
+            codes = pool.tile([P, PASSES, n], U32, name="h_codes%s" % c, align_bytes=256)
+            planes = pool.tile([P, PASSES, n], U8, name="h_planes%s" % c, align_bytes=256)
             nc.vector.quantize_mx(
                 out=codes[:].rearrange("p o j -> p (o j)").bitcast(FP8X4),
                 scales=planes[:].rearrange("p o j -> p (o j)"),
@@ -122,8 +122,8 @@ def tile_picked_zdeja_relu2_po_kernel(tc, x_words, x_scales, hT, offs, out_0, ou
 
         def quantize_one(c, o, offset):
             n = CHUNKS[c][1]
-            codes = reuse.tile([P, n], U32, name="h_codes%s%d" % (c, o), align_bytes=64, offset=offset)
-            planes = pool.tile([P, n], U8, name="h_planes%s%d" % (c, o), align_bytes=64)
+            codes = reuse.tile([P, n], U32, name="h_codes%s%d" % (c, o), align_bytes=256, offset=offset)
+            planes = pool.tile([P, n], U8, name="h_planes%s%d" % (c, o), align_bytes=256)
             nc.vector.quantize_mx(out=codes[:].bitcast(FP8X4), scales=planes[:], in_=h_woven[c][:, o].rearrange("p j t -> p (j t)"))
             h_codes[(c, o)] = codes[:]
             h_planes[(c, o)] = planes[:]
@@ -159,7 +159,7 @@ def tile_picked_zdeja_relu2_po_kernel(tc, x_words, x_scales, hT, offs, out_0, ou
                 )
 
         relu = {}
-        relu_offset = {("a", 0): 10 * KIB - 64, ("a", 1): 12 * KIB - 128, ("b", 0): 8 * KIB + 64, ("b", 1): 22 * KIB, ("c", 0): 52 * KIB, ("c", 1): 56 * KIB}
+        relu_offset = {("a", 0): 10 * KIB - 256, ("a", 1): 12 * KIB - 512, ("b", 0): 8 * KIB + 256, ("b", 1): 22 * KIB, ("c", 0): 52 * KIB, ("c", 1): 56 * KIB}
         y = {}
         for half in range(2):
             for g in range(1 - half, GROUPS):
@@ -177,7 +177,7 @@ def tile_picked_zdeja_relu2_po_kernel(tc, x_words, x_scales, hT, offs, out_0, ou
             n = CHUNKS[c][1]
             b, col = place[(c, g, t)]
             if (c, g) not in relu:
-                relu[(c, g)] = reuse.tile([P, PACK, n], F32, name="relu%s%d" % (c, g), align_bytes=64, offset=relu_offset[(c, g)])
+                relu[(c, g)] = reuse.tile([P, PACK, n], F32, name="relu%s%d" % (c, g), align_bytes=256, offset=relu_offset[(c, g)])
             dst, src = relu[(c, g)][:, t : t + rows, :].rearrange("p t j -> p (t j)"), banks[b][:, col : col + rows * n]
             if on_scalar:
                 nc.scalar.activation(dst, src, ACT.Relu)
@@ -196,28 +196,24 @@ def tile_picked_zdeja_relu2_po_kernel(tc, x_words, x_scales, hT, offs, out_0, ou
             nc.sync.dma_start(y_rows[g][:, t : t + rows, first : first + n], y_view(c, g, t, rows))
 
         y_woven = {}
-        y_codes = [pool.tile([P, GROUPS, HALF], U32, name="y_codes%d" % half, align_bytes=256) for half in range(2)]
+        y_codes = [pool.tile([P, J], U32, name="y_codes%d" % g, align_bytes=256) for g in range(GROUPS)]
 
         def weave_part(c):
             first, n = CHUNKS[c]
             weave(False, y_woven[(0, 0)][:, first : first + n, :], y_first[c][:])
 
         def weave_y(half, g, scalar_cols):
-            y_woven[(half, g)] = pool.tile([P, HALF, PACK], BF16, name="y_woven%d%d" % (half, g), align_bytes=64)
+            y_woven[(half, g)] = pool.tile([P, HALF, PACK], BF16, name="y_woven%d%d" % (half, g), align_bytes=256)
             if scalar_cols > 0:
                 weave(True, y_woven[(half, g)][:, :scalar_cols, :], y[(half, g)][:, :, :scalar_cols])
             weave(False, y_woven[(half, g)][:, scalar_cols:, :], y[(half, g)][:, :, scalar_cols:])
 
         def hand_on(half, g):
             cols = slice(half * HALF, (half + 1) * HALF)
-            nc.vector.quantize_mx(out=y_codes[half][:, g, :].bitcast(FP8X4), scales=y_planes[4 * g : P, cols], in_=y_woven[(half, g)][:].rearrange("p j t -> p (j t)"))
+            nc.vector.quantize_mx(out=y_codes[g][:, cols].bitcast(FP8X4), scales=y_planes[:, g, cols], in_=y_woven[(half, g)][:].rearrange("p j t -> p (j t)"))
 
-        def store_codes(half, g, groups):
-            cols = slice(half * HALF, (half + 1) * HALF)
-            nc.sync.dma_start(
-                out_1[g : g + groups, :, cols, :].rearrange("g p j t -> p g (j t)").bitcast(I32),
-                y_codes[half][:, g : g + groups, :].bitcast(I32),
-            )
+        def store_codes(g, lo, hi):
+            nc.sync.dma_start(out_1[g, :, lo:hi, :].rearrange("p j t -> p (j t)").bitcast(I32), y_codes[g][:, lo:hi].bitcast(I32))
 
         nc.vector.tensor_copy(scale_picked[:, :S], scale_win[:].indirect(offsets[:]))
         nc.vector.tensor_copy(scale_dealt[:], scale_picked[:, :S].rearrange("p (g m t) -> p g t m", g=GROUPS, t=PACK))
@@ -230,13 +226,13 @@ def tile_picked_zdeja_relu2_po_kernel(tc, x_words, x_scales, hT, offs, out_0, ou
             for o in range(PASSES):
                 if (c, o) not in h_raw:
                     load_h(c, o)
-        early_codes = reuse.tile([P, GROUPS, PACK, P], U32, name="early_codes", align_bytes=64, offset=40 * KIB)
+        early_codes = reuse.tile([P, GROUPS, PACK, P], U32, name="early_codes", align_bytes=256, offset=40 * KIB)
         nc.vector.tensor_copy(early_codes[:].rearrange("p g t m -> p g m t"), word_win[1][:].indirect(offsets[:]))
         for g in range(GROUPS):
             x_codes[(1, g)] = early_codes[:, g]
-        h_woven["a"] = reuse.tile([P, PASSES, 128, PACK], BF16, name="h_woven_a", align_bytes=64, offset=24 * KIB)
-        h_woven["b"] = pool.tile([P, PASSES, 128, PACK], BF16, name="h_woven_b", align_bytes=64)
-        h_woven["c"] = reuse.tile([P, PASSES, 256, PACK], BF16, name="h_woven_c", align_bytes=64, offset=4 * KIB + 64)
+        h_woven["a"] = reuse.tile([P, PASSES, 128, PACK], BF16, name="h_woven_a", align_bytes=256, offset=24 * KIB)
+        h_woven["b"] = pool.tile([P, PASSES, 128, PACK], BF16, name="h_woven_b", align_bytes=256)
+        h_woven["c"] = reuse.tile([P, PASSES, 256, PACK], BF16, name="h_woven_c", align_bytes=256, offset=4 * KIB + 256)
         for o in range(PASSES):
             weave_h("a", o, 128)
             quantize_one("a", o, (50 + o) * KIB)
@@ -271,42 +267,41 @@ def tile_picked_zdeja_relu2_po_kernel(tc, x_words, x_scales, hT, offs, out_0, ou
         square(True, "a", 0, 2, 2)
         store_y("a", 0, 0, 4)
         rectify(True, "a", 1, 0, 4)
-        multiply("c", 0)
         multiply("c", 1)
+        multiply("c", 0)
         rectify(True, "b", 0, 0, 4)
         square(True, "a", 1, 0, 4)
         store_y("a", 1, 0, 4)
         rectify(False, "b", 1, 0, 4)
-        y_woven[(0, 0)] = reuse.tile([P, HALF, PACK], BF16, name="y_woven00", align_bytes=64, offset=20 * KIB)
+        y_woven[(0, 0)] = reuse.tile([P, HALF, PACK], BF16, name="y_woven00", align_bytes=256, offset=20 * KIB)
         weave_part("a")
         square(True, "b", 0, 0, 4)
         store_y("b", 0, 0, 4)
         square(True, "b", 1, 0, 4)
         store_y("b", 1, 0, 4)
-        rectify(False, "c", 0, 0, 2)
-        rectify(True, "c", 0, 2, 2)
+        rectify(False, "c", 1, 0, 2)
+        rectify(True, "c", 1, 2, 2)
         weave_part("b")
-        square(False, "c", 0, 0, 2)
-        store_y("c", 0, 0, 2)
-        rectify(True, "c", 1, 0, 2)
-        hand_on(0, 0)
-        store_codes(0, 0, 1)
-        square(True, "c", 0, 2, 2)
-        store_y("c", 0, 2, 2)
-        rectify(False, "c", 1, 2, 2)
-        square(True, "c", 1, 0, 2)
+        square(False, "c", 1, 0, 2)
         store_y("c", 1, 0, 2)
-        weave_y(0, 1, 0)
+        rectify(True, "c", 0, 0, 2)
+        hand_on(0, 0)
+        store_codes(0, 0, HALF)
         square(True, "c", 1, 2, 2)
         store_y("c", 1, 2, 2)
-        weave_y(1, 0, 0)
+        rectify(False, "c", 0, 2, 2)
+        square(True, "c", 0, 0, 2)
+        store_y("c", 0, 0, 2)
+        weave_y(0, 1, 0)
+        square(True, "c", 0, 2, 2)
+        store_y("c", 0, 2, 2)
+        weave_y(1, 1, 0)
         hand_on(0, 1)
-        store_codes(0, 1, 1)
-        weave_y(1, 1, 160)
-        hand_on(1, 0)
-        store_codes(1, 0, 1)
+        weave_y(1, 0, 160)
         hand_on(1, 1)
-        store_codes(1, 1, 1)
+        store_codes(1, 0, J)
+        hand_on(1, 0)
+        store_codes(0, HALF, J)
         for q in range(QUADS):
-            queue = nc.scalar if q == 0 else nc.sync
-            queue.dma_start(out_2[:, 4 * q : 4 * q + 4, :].bitcast(I32), y_planes[32 * q : 32 * q + 8, :].bitcast(I32))
+            queue = nc.scalar if q < 2 else nc.sync
+            queue.dma_start(out_2[:, 4 * q : 4 * q + 4, :].rearrange("g r j -> r g j").bitcast(I32), y_planes[32 * q : 32 * q + 4].bitcast(I32))

@@ -159,7 +159,7 @@ def tile_picked_zdeja_relu2_po_kernel(tc, x_words, x_scales, hT, offs, out_0, ou
                 )
 
         relu = {}
-        relu_offset = {("a", 0): 10 * KIB - 256, ("a", 1): 12 * KIB - 512, ("b", 0): 8 * KIB + 256, ("b", 1): 22 * KIB, ("c", 0): 52 * KIB, ("c", 1): 56 * KIB}
+        relu_offset = {("a", 0): 12 * KIB + 256, ("a", 1): 10 * KIB + 512, ("b", 0): 14 * KIB, ("b", 1): 22 * KIB, ("c", 0): 52 * KIB, ("c", 1): 56 * KIB}
         y = {}
         for half in range(2):
             for g in range(1 - half, GROUPS):
@@ -258,9 +258,19 @@ def tile_picked_zdeja_relu2_po_kernel(tc, x_words, x_scales, hT, offs, out_0, ou
         multiply("b", 0)
         multiply("b", 1)
         weave_h("c", 0, 0)
-        weave_h("c", 1, 0)
         quantize_one("c", 0, 48 * KIB)
-        quantize_one("c", 1, 49 * KIB)
+        last_codes = pool.tile([P, 256], U32, name="last_codes", align_bytes=256)
+        last_planes = pool.tile([P, 256], U8, name="last_planes", align_bytes=256)
+        for lo in (0, 128):
+            weave(False, h_woven["c"][:, 1, lo : lo + 128, :], h_raw[("c", 1)][:, :, lo : lo + 128])
+        for lo in (0, 128):
+            nc.vector.quantize_mx(
+                out=last_codes[:, lo : lo + 128].bitcast(FP8X4),
+                scales=last_planes[:, lo : lo + 128],
+                in_=h_woven["c"][:, 1, lo : lo + 128, :].rearrange("p j t -> p (j t)"),
+            )
+        h_codes[("c", 1)] = last_codes[:]
+        h_planes[("c", 1)] = last_planes[:]
         rectify(True, "a", 0, 0, 2)
         rectify(True, "a", 0, 2, 2)
         square(True, "a", 0, 0, 2)
@@ -297,9 +307,9 @@ def tile_picked_zdeja_relu2_po_kernel(tc, x_words, x_scales, hT, offs, out_0, ou
         store_y("c", 0, 2, 2)
         weave_y(1, 1, 0)
         hand_on(0, 1)
-        weave_y(1, 0, 160)
         hand_on(1, 1)
         store_codes(1, 0, J)
+        weave_y(1, 0, 128)
         hand_on(1, 0)
         store_codes(0, HALF, J)
         for q in range(QUADS):

@@ -236,16 +236,6 @@ def tile_picked_zdeja_relu2_po_kernel(tc, x_words, x_scales, hT, offs, out_0, ou
         for o in range(PASSES):
             weave_h("a", o, 128)
             quantize_one("a", o, (50 + o) * KIB)
-        for n in (512, 256):
-            nc.tensor.matmul_mx(
-                out=banks[7][:, :n],
-                lhsT=h_codes[("a", 1)].bitcast(FP8X4),
-                lhsT_scale=h_planes[("a", 1)],
-                rhs=x_codes[(1, 0)].rearrange("p t m -> p (t m)")[:, :n].bitcast(FP8X4),
-                rhs_scale=scale_dealt[:, 0].rearrange("p t m -> p (t m)")[:, :n],
-                start=True,
-                stop=True,
-            )
         multiply_first(0, 1)
         gather_words(0, 0, 44 * KIB)
         multiply_first(0, 0)

@@ -299,7 +299,7 @@ def tile_picked_zdeja_relu2_po_kernel(tc, x_words, x_scales, hT, offs, out_0, ou
         hand_on(0, 1)
         hand_on(1, 1)
         store_codes(1, 0, J)
-        weave_y(1, 0, 128)
+        weave_y(1, 0, 192)
         hand_on(1, 0)
         store_codes(0, HALF, J)
         for q in range(QUADS):

from contextlib import ExitStack

import concourse.mybir as mybir

K, T, S, J = 1024, 4096, 1024, 512
FLOPS = 2 * K * S * J

F32 = mybir.dt.float32
BF16 = mybir.dt.bfloat16
I32 = mybir.dt.int32
U32 = mybir.dt.uint32
U16 = mybir.dt.uint16
U8 = mybir.dt.uint8
FP8X4 = mybir.dt.float8_e4m3fn_x4
ACT = mybir.ActivationFunctionType
ALU = mybir.AluOpType

P = 128
PACK = 4
PASSES = 2
GROUPS = 2
GROUP = 512
QUADS = 4
BANK = 512
CHUNKS = {"a": (0, 128), "b": (128, 128), "c": (256, 256)}
HALF = 256
KIB = 1024
LATE_SPLIT = 1792


def weave_views(dst, src):
    return (dst.rearrange("p (c i) t -> p c t i", i=4), src.rearrange("p t (c i) -> p c t i", i=4))


def tile_picked_zdeja_relu2_po_kernel(tc, x_words, x_scales, hT, offs, out_0, out_1, out_2):
    nc = tc.nc
    with ExitStack() as ctx:
        pool = ctx.enter_context(tc.tile_pool(name="keep", bufs=1))
        reuse = ctx.enter_context(tc.tile_pool(name="reuse", bufs=1))
        psum = ctx.enter_context(tc.psum_pool(name="psum", bufs=1))

        offsets = pool.tile([P, S // 16], U16, name="offsets")
        word_win = [pool.tile([P, T], U32, name="word_win%d" % o, align_bytes=256) for o in range(PASSES)]
        scale_win = pool.tile([P, T], U8, name="scale_win", align_bytes=256)

        nc.vector.memset(scale_win[:].bitcast(I32), 0)

        def load_words(o, lo, hi):
            nc.sync.dma_start(word_win[o][:, lo:hi].bitcast(I32), x_words[o][:, lo:hi, :].rearrange("p n t -> p (n t)").bitcast(I32))

        h_rows = hT.rearrange("(o p t) j -> o p t j", p=P, t=PACK)
        h_raw = {}

        raw_offset = {("a", 0): 0, ("a", 1): 2 * KIB, ("b", 0): 14 * KIB, ("b", 1): 8 * KIB, ("c", 0): 16 * KIB, ("c", 1): 20 * KIB}

        def load_h(c, o):
            first, n = CHUNKS[c]
            h_raw[(c, o)] = reuse.tile([P, PACK, n], F32, name="h_raw%s%d" % (c, o), align_bytes=256, offset=raw_offset[(c, o)])
            nc.sync.dma_start(h_raw[(c, o)][:], h_rows[o][:, :, first : first + n])

        load_h("a", 0)
        load_words(0, 0, LATE_SPLIT)
        nc.sync.dma_start(offsets[:], offs)
        nc.sync.dma_start(scale_win[32:96:2, :].bitcast(I32), x_scales.rearrange("o r n -> r o n").bitcast(I32))
        load_words(1, 0, T)
        load_h("a", 1)
        load_words(0, LATE_SPLIT, T)

        x_codes = {}
        scale_picked = reuse.tile([P, 20 * KIB], U8, name="scale_picked", align_bytes=256, offset=4 * KIB)
        scale_dealt = pool.tile([P, GROUPS, PACK, P], U8, name="scale_dealt", align_bytes=256)
        x_planes = pool.tile([P, GROUPS, PACK, P], U8, name="x_planes", align_bytes=256)

        def gather_words(o, g, offset):
            x_codes[(o, g)] = reuse.tile([P, PACK, P], U32, name="x_codes%d%d" % (o, g), align_bytes=256, offset=offset)
            nc.vector.tensor_copy(
                x_codes[(o, g)][:].rearrange("p t m -> p m t"),
                word_win[o][:].indirect(offsets[:, g * (GROUP // 16) : (g + 1) * (GROUP // 16)]),
            )

        h_woven = {}
        h_codes = {}
        h_planes = {}
        banks = [psum.tile([P, BANK], F32, name="bank%d" % b) for b in range(8)]
        place = {}
        for t in range(PACK):
            place[("a", 0, t)] = (t // 2, (t % 2) * 128)
            place[("a", 1, t)] = (2, t * 128)
            place[("b", 0, t)] = (3, t * 128)
            place[("b", 1, t)] = (4, t * 128)
            place[("c", 1, t)] = (5 + t // 2, (t % 2) * 256)
            place[("c", 0, t)] = ((7 + t // 2) % 8, (t % 2) * 256)
        y_planes = pool.tile([P, GROUPS, J], U8, name="y_planes", align_bytes=256)
        y_rows = out_0.rearrange("(g p t) j -> g p t j", p=P, t=PACK)

        def weave(on_scalar, dst, src):
            dst, src = weave_views(dst, src)
            if on_scalar:
                nc.scalar.activation(dst, src, ACT.Copy)
            else:
                nc.vector.tensor_copy(dst, src)

        def weave_h(c, o, scalar_cols):
            n = CHUNKS[c][1]
            if scalar_cols > 0:
                weave(True, h_woven[c][:, o, :scalar_cols, :], h_raw[(c, o)][:, :, :scalar_cols])
            if scalar_cols < n:
                weave(False, h_woven[c][:, o, scalar_cols:, :], h_raw[(c, o)][:, :, scalar_cols:])

        def quantize_both(c):
            n = CHUNKS[c][1]
            codes = pool.tile([P, PASSES, n], U32, name="h_codes%s" % c, align_bytes=256)
            planes = pool.tile([P, PASSES, n], U8, name="h_planes%s" % c, align_bytes=256)
            nc.vector.quantize_mx(
                out=codes[:].rearrange("p o j -> p (o j)").bitcast(FP8X4),
                scales=planes[:].rearrange("p o j -> p (o j)"),
                in_=h_woven[c][:].rearrange("p o j t -> p (o j t)"),
            )
            for o in range(PASSES):
                h_codes[(c, o)] = codes[:, o, :]
                h_planes[(c, o)] = planes[:, o, :]

        def quantize_one(c, o, offset):
            n = CHUNKS[c][1]
            codes = reuse.tile([P, n], U32, name="h_codes%s%d" % (c, o), align_bytes=256, offset=offset)
            planes = pool.tile([P, n], U8, name="h_planes%s%d" % (c, o), align_bytes=256)
            nc.vector.quantize_mx(out=codes[:].bitcast(FP8X4), scales=planes[:], in_=h_woven[c][:, o].rearrange("p j t -> p (j t)"))
            h_codes[(c, o)] = codes[:]
            h_planes[(c, o)] = planes[:]

        def multiply(c, g):
            n = CHUNKS[c][1]
            for t in range(PACK):
                b, col = place[(c, g, t)]
                order = (0, 1)
                for o in order:
                    nc.tensor.matmul_mx(
                        out=banks[b][:, col : col + n],
                        lhsT=x_codes[(o, g)][:, t, :].bitcast(FP8X4),
                        lhsT_scale=x_planes[4 * o : P, g, t, :],
                        rhs=h_codes[(c, o)].bitcast(FP8X4),
                        rhs_scale=h_planes[(c, o)],
                        start=(o == order[0]),
                        stop=(o == order[1]),
                    )

        def multiply_first(g, o):
            for t in range(PACK):
                b, col = place[("a", g, t)]
                last = col + 128 == (256 if g == 0 else 512)
                nc.tensor.matmul_mx(
                    out=banks[b][:, col : col + 128],
                    lhsT=x_codes[(o, g)][:, t, :].bitcast(FP8X4),
                    lhsT_scale=x_planes[4 * o : P, g, t, :],
                    rhs=h_codes[("a", o)].bitcast(FP8X4),
                    rhs_scale=h_planes[("a", o)],
                    start=(o == 1 and col == 0),
                    stop=(o == 0 and last),
                )

        relu = {}
        relu_offset = {("a", 0): 12 * KIB + 256, ("a", 1): 10 * KIB + 512, ("b", 0): 14 * KIB, ("b", 1): 22 * KIB, ("c", 0): 52 * KIB, ("c", 1): 56 * KIB}
        y = {}
        for half in range(2):
            for g in range(1 - half, GROUPS):
                y[(half, g)] = pool.tile([P, PACK, HALF], F32, name="y%d%d" % (half, g), align_bytes=256)

        y_first = {c: pool.tile([P, PACK, 128], F32, name="y_first%s" % c, align_bytes=256) for c in "ab"}

        def y_view(c, g, t, rows):
            first, n = CHUNKS[c]
            if g == 0 and c in y_first:
                return y_first[c][:, t : t + rows, :]
            return y[(first // HALF, g)][:, t : t + rows, first % HALF : first % HALF + n]

        def rectify(on_scalar, c, g, t, rows):
            n = CHUNKS[c][1]
            b, col = place[(c, g, t)]
            if (c, g) not in relu:
                relu[(c, g)] = reuse.tile([P, PACK, n], F32, name="relu%s%d" % (c, g), align_bytes=256, offset=relu_offset[(c, g)])
            dst, src = relu[(c, g)][:, t : t + rows, :].rearrange("p t j -> p (t j)"), banks[b][:, col : col + rows * n]
            if on_scalar:
                nc.scalar.activation(dst, src, ACT.Relu)
            else:
                nc.vector.tensor_scalar(dst, src, 0.0, None, ALU.max)

        def square(on_scalar, c, g, t, rows):
            dst, src = y_view(c, g, t, rows), relu[(c, g)][:, t : t + rows, :]
            if on_scalar:
                nc.scalar.activation(dst, src, ACT.Square)
            else:
                nc.vector.tensor_tensor(dst, src, src, ALU.mult)

        def store_y(c, g, t, rows):
            first, n = CHUNKS[c]
            nc.sync.dma_start(y_rows[g][:, t : t + rows, first : first + n], y_view(c, g, t, rows))

        y_woven = {}
        y_codes = [pool.tile([P, J], U32, name="y_codes%d" % g, align_bytes=256) for g in range(GROUPS)]

        def weave_part(c):
            first, n = CHUNKS[c]
            weave(False, y_woven[(0, 0)][:, first : first + n, :], y_first[c][:])

        def weave_y(half, g, scalar_cols):
            y_woven[(half, g)] = pool.tile([P, HALF, PACK], BF16, name="y_woven%d%d" % (half, g), align_bytes=256)
            if scalar_cols > 0:
                weave(True, y_woven[(half, g)][:, :scalar_cols, :], y[(half, g)][:, :, :scalar_cols])
            weave(False, y_woven[(half, g)][:, scalar_cols:, :], y[(half, g)][:, :, scalar_cols:])

        def hand_on(half, g):
            cols = slice(half * HALF, (half + 1) * HALF)
            nc.vector.quantize_mx(out=y_codes[g][:, cols].bitcast(FP8X4), scales=y_planes[:, g, cols], in_=y_woven[(half, g)][:].rearrange("p j t -> p (j t)"))

        def store_codes(g, lo, hi):
            nc.sync.dma_start(out_1[g, :, lo:hi, :].rearrange("p j t -> p (j t)").bitcast(I32), y_codes[g][:, lo:hi].bitcast(I32))

        nc.vector.tensor_copy(scale_picked[:, :S], scale_win[:].indirect(offsets[:]))
        nc.vector.tensor_copy(scale_dealt[:], scale_picked[:, :S].rearrange("p (g m t) -> p g t m", g=GROUPS, t=PACK))
        for r in range(4):
            nc.sync.dma_start(
                x_planes[r:P:4].rearrange("p g t m -> p (g t m)").bitcast(I32),
                scale_dealt[32 + 4 * r : 96 + 4 * r : 2].rearrange("p g t m -> p (g t m)").bitcast(I32),
            )
        for c in CHUNKS:
            for o in range(PASSES):
                if (c, o) not in h_raw:
                    load_h(c, o)
        early_codes = reuse.tile([P, GROUPS, PACK, P], U32, name="early_codes", align_bytes=256, offset=40 * KIB)
        nc.vector.tensor_copy(early_codes[:].rearrange("p g t m -> p g m t"), word_win[1][:].indirect(offsets[:]))
        for g in range(GROUPS):
            x_codes[(1, g)] = early_codes[:, g]
        h_woven["a"] = reuse.tile([P, PASSES, 128, PACK], BF16, name="h_woven_a", align_bytes=256, offset=24 * KIB)
        h_woven["b"] = pool.tile([P, PASSES, 128, PACK], BF16, name="h_woven_b", align_bytes=256)
        h_woven["c"] = reuse.tile([P, PASSES, 256, PACK], BF16, name="h_woven_c", align_bytes=256, offset=4 * KIB + 256)
        for o in range(PASSES):
            weave_h("a", o, 128)
            quantize_one("a", o, (50 + o) * KIB)
        multiply_first(0, 1)
        gather_words(0, 0, 44 * KIB)
        multiply_first(0, 0)
        multiply_first(1, 1)
        gather_words(0, 1, 46 * KIB)
        multiply_first(1, 0)
        weave_h("b", 0, 128)
        weave_h("b", 1, 128)
        quantize_both("b")
        multiply("b", 0)
        multiply("b", 1)
        weave_h("c", 0, 0)
        quantize_one("c", 0, 48 * KIB)
        last_codes = pool.tile([P, 256], U32, name="last_codes", align_bytes=256)
        last_planes = pool.tile([P, 256], U8, name="last_planes", align_bytes=256)
        for lo in (0, 128):
            weave(False, h_woven["c"][:, 1, lo : lo + 128, :], h_raw[("c", 1)][:, :, lo : lo + 128])
        for lo in (0, 128):
            nc.vector.quantize_mx(
                out=last_codes[:, lo : lo + 128].bitcast(FP8X4),
                scales=last_planes[:, lo : lo + 128],
                in_=h_woven["c"][:, 1, lo : lo + 128, :].rearrange("p j t -> p (j t)"),
            )
        h_codes[("c", 1)] = last_codes[:]
        h_planes[("c", 1)] = last_planes[:]
        rectify(True, "a", 0, 0, 2)
        rectify(True, "a", 0, 2, 2)
        square(True, "a", 0, 0, 2)
        square(True, "a", 0, 2, 2)
        store_y("a", 0, 0, 4)
        rectify(True, "a", 1, 0, 4)
        multiply("c", 1)
        multiply("c", 0)
        rectify(True, "b", 0, 0, 4)
        square(True, "a", 1, 0, 4)
        store_y("a", 1, 0, 4)
        rectify(False, "b", 1, 0, 4)
        y_woven[(0, 0)] = reuse.tile([P, HALF, PACK], BF16, name="y_woven00", align_bytes=256, offset=20 * KIB)
        weave_part("a")
        square(True, "b", 0, 0, 4)
        store_y("b", 0, 0, 4)
        square(True, "b", 1, 0, 4)
        store_y("b", 1, 0, 4)
        rectify(False, "c", 1, 0, 2)
        rectify(True, "c", 1, 2, 2)
        weave_part("b")
        square(False, "c", 1, 0, 2)
        store_y("c", 1, 0, 2)
        rectify(True, "c", 0, 0, 2)
        hand_on(0, 0)
        store_codes(0, 0, HALF)
        square(True, "c", 1, 2, 2)
        store_y("c", 1, 2, 2)
        rectify(False, "c", 0, 2, 2)
        square(True, "c", 0, 0, 2)
        store_y("c", 0, 0, 2)
        weave_y(0, 1, 0)
        square(True, "c", 0, 2, 2)
        store_y("c", 0, 2, 2)
        weave_y(1, 1, 0)
        hand_on(0, 1)
        hand_on(1, 1)
        store_codes(1, 0, J)
        weave_y(1, 0, 192)
        hand_on(1, 0)
        store_codes(0, HALF, J)
        for q in range(QUADS):
            queue = nc.scalar if q < 2 else nc.sync
            queue.dma_start(out_2[:, 4 * q : 4 * q + 4, :].rearrange("g r j -> r g j").bitcast(I32), y_planes[32 * q : 32 * q + 4].bitcast(I32))
